import numpy as np
import ml_dtypes


def mxq(x, axis, fmt="e4m3"):
    dtype, down = {"e4m3": (ml_dtypes.float8_e4m3fn, 7), "e5m2": (ml_dtypes.float8_e5m2, 14)}[fmt]
    v = np.moveaxis(np.asarray(x, np.float32).astype(ml_dtypes.bfloat16).astype(np.float64), axis, -1)
    blocks = v.reshape(v.shape[:-1] + (-1, 32))
    amax = np.abs(blocks).max(-1, keepdims=True)
    byte = np.maximum(np.where(amax > 0, np.frexp(amax)[1] - 1 + 127, 0) - down, 1)
    scale = np.exp2(byte - 127.0)
    codes = (blocks / scale).astype(np.float32).astype(dtype).astype(np.float64)
    return np.moveaxis((codes * scale).reshape(v.shape), -1, axis)


WIDE = False


def mx_kscale(k):
    if not WIDE:
        return np.ones(k)
    levels = np.array([10, -10, 5, -5, 0])
    if k % 512:
        return np.exp2(np.random.permutation(np.resize(levels, k // 32))).repeat(32)
    a = np.empty((k // 512, 16))
    for p in range(k // 512):
        a[p, :8] = np.random.permutation(np.resize(levels, 8))
        for g in range(8):
            far = levels[np.abs(levels - a[p, g]) >= 10]
            a[p, g + 8] = far[np.random.randint(len(far))]
    return np.exp2(a.ravel()).repeat(32)


def f64(x):
    return np.asarray(x).astype(np.float64)


def striped(idx):
    return np.tile(idx.reshape(-1, 16).T, (8, 1)).astype(np.uint16)


def unstriped(offs):
    return offs[:16].T.reshape(-1).astype(np.int64)


def pack_weight(w):
    k, n = w.shape
    w = f64(np.asarray(w, np.float32).astype(ml_dtypes.bfloat16)).reshape(k // 32, 32, n)
    amax = np.abs(w).max(1)
    byte = np.clip(np.where(amax > 0, np.frexp(amax)[1] - 1 + 127 - 7, 1), 1, 254)
    scaled = (w * np.exp2(127.0 - byte)[:, None, :]).reshape(k, n).astype(np.float32)
    words = np.ascontiguousarray(scaled.reshape(k // 512, 128, 4, n).transpose(0, 1, 3, 2)).astype(ml_dtypes.float8_e4m3fn).view(np.uint8)
    return words, np.ascontiguousarray(byte.astype(np.uint8).reshape(k // 512, 16, n))


def unpack_weight(words, scales):
    g, p, n, _ = words.shape
    vals = np.ascontiguousarray(words).view(ml_dtypes.float8_e4m3fn).astype(np.float64) * np.repeat(np.exp2(scales.astype(np.float64) - 127.0), 8, axis=1)[..., None]
    return vals.transpose(0, 1, 3, 2).reshape(g * 512, n)


K, T, S, N = 1024, 4096, 1024, 256
P = 2 ** 7


def setup_inputs():
    n = np.random.standard_normal
    s = mx_kscale(K)[:, None]
    turn = np.random.uniform(0.0, 2.0 * np.pi, (N // 2, T))
    packed_xT = pack_weight(n((K, T)) * s)
    return {
        "x_words": packed_xT[0],
        "x_scales": packed_xT[1],
        "w1": (n((K, N)) / np.sqrt(K) / s).astype(np.float32),
        "ct": (np.tile(np.cos(turn), (2, 1))).astype(np.float32),
        "st": (np.tile(np.sin(turn), (2, 1))).astype(np.float32),
        "offs": striped(np.random.permutation(T)[:S]),
    }


def reference(x_words, x_scales, w1, ct, st, offs):
    xq = unpack_weight(x_words, x_scales)[:, unstriped(offs)]
    y = mxq(f64(w1), 0, "e4m3").T @ xq
    cs = f64(ct)[:, unstriped(offs)]
    sn = f64(st)[:, unstriped(offs)]
    return y * cs + np.concatenate([-y[P:], y[:P]]) * sn

@@ -1,0 +1,126 @@
+from contextlib import ExitStack
+
+import concourse.mybir as mybir
+
+K, T, S, N = 1024, 4096, 1024, 256
+FLOPS = 2 * K * S * N
+P = 128
+PACK = 4
+PASSES = K // (P * PACK)
+HALVES = N // P
+CH = 512
+CHUNKS = S // CH
+
+F32 = mybir.dt.float32
+BF16 = mybir.dt.bfloat16
+I32 = mybir.dt.int32
+U32 = mybir.dt.uint32
+U16 = mybir.dt.uint16
+U8 = mybir.dt.uint8
+FP8X4 = mybir.dt.float8_e4m3fn_x4
+MULT = mybir.AluOpType.mult
+ADD = mybir.AluOpType.add
+SUB = mybir.AluOpType.subtract
+
+
+def tile_picked_zrope_none_p_kernel(tc, x_words, x_scales, w1, ct, st, offs, out):
+    nc = tc.nc
+    with ExitStack() as ctx:
+        keep = ctx.enter_context(tc.tile_pool(name="keep", bufs=1))
+        psum = ctx.enter_context(tc.psum_pool(name="psum", bufs=1))
+
+        offsets = keep.tile([P, S // 16], U16, name="offsets")
+        nc.sync.dma_start(offsets[:], offs)
+
+        scale_rows = keep.tile([P, T], U8, name="scale_rows", align_bytes=64)
+        x_planes = keep.tile([P, S], U8, name="x_planes", align_bytes=64)
+        nc.vector.memset(scale_rows[:].bitcast(I32), 0)
+        nc.vector.memset(x_planes[:].bitcast(I32), 0)
+        nc.scalar.dma_start(
+            out=scale_rows[0:P:4, :].bitcast(I32),
+            in_=x_scales.rearrange("o q c -> (o q) c").bitcast(I32),
+        )
+
+        w_raw = keep.tile([P, PASSES, PACK, N], F32, name="w_raw")
+        nc.sync.dma_start(
+            out=w_raw[:].rearrange("p o j n -> p o (j n)"),
+            in_=w1.rearrange("(o p j) n -> p o (j n)", o=PASSES, j=PACK),
+        )
+        words = []
+        for o in range(PASSES):
+            t = keep.tile([P, T], U32, name="words%d" % o, align_bytes=64)
+            nc.sync.dma_start(
+                out=t[:].bitcast(I32),
+                in_=x_words[o].rearrange("p c r -> p (c r)").bitcast(I32),
+            )
+            words.append(t)
+        cos_rows = keep.tile([P, T], F32, name="cos_rows", align_bytes=64)
+        nc.sync.dma_start(out=cos_rows[:], in_=ct[0:P, :])
+        sin_rows = keep.tile([P, T], F32, name="sin_rows", align_bytes=64)
+        nc.sync.dma_start(out=sin_rows[:], in_=st[0:P, :])
+
+        picked_rows = keep.tile([P, S], U8, name="picked_rows", align_bytes=64)
+        nc.vector.tensor_copy(picked_rows[:], scale_rows[:].indirect(offsets[:]))
+        for o in range(PASSES):
+            for q in range(4):
+                src = 64 * o + 16 * q
+                dst = 32 * q + 4 * o
+                nc.gpsimd.dma_start(
+                    out=x_planes[dst : dst + 4, :].bitcast(I32),
+                    in_=picked_rows[src : src + 13 : 4, :].bitcast(I32),
+                )
+
+        w_grouped = keep.tile([P, PASSES, N, PACK], BF16, name="w_grouped", align_bytes=64)
+        for o in range(PASSES):
+            nc.scalar.copy(out=w_grouped[:, o], in_=w_raw[:, o].rearrange("p j n -> p n j"))
+        w_codes = keep.tile([P, PASSES * N], U32, name="w_codes", align_bytes=64)
+        w_planes = keep.tile([P, PASSES * N], U8, name="w_planes", align_bytes=64)
+        nc.vector.quantize_mx(
+            out=w_codes[:].bitcast(FP8X4),
+            scales=w_planes[:],
+            in_=w_grouped[:].rearrange("p o n j -> p (o n j)"),
+        )
+
+        picked = []
+        for o in range(PASSES):
+            t = keep.tile([P, S], U32, name="picked%d" % o, align_bytes=64)
+            nc.vector.tensor_copy(t[:], words[o][:].indirect(offsets[:]))
+            picked.append(t)
+
+        y = {}
+        for c in range(CHUNKS):
+            cols = slice(c * CH, (c + 1) * CH)
+            for h in range(HALVES):
+                y[c, h] = psum.tile([P, CH], F32, name="y%d%d" % (c, h))
+                for o in range(PASSES):
+                    wc = slice(o * N + h * P, o * N + (h + 1) * P)
+                    nc.tensor.matmul_mx(
+                        out=y[c, h][:],
+                        lhsT=w_codes[:, wc].bitcast(FP8X4),
+                        lhsT_scale=w_planes[:, wc],
+                        rhs=picked[o][:, cols].bitcast(FP8X4),
+                        rhs_scale=x_planes[4 * o :, cols],
+                        start=(o == 0),
+                        stop=(o == PASSES - 1),
+                    )
+
+        prods = {}
+        for nm, rows in (("cos", cos_rows), ("sin", sin_rows)):
+            got = []
+            for c in range(CHUNKS):
+                g = keep.tile([P, CH], F32, name="%s_picked%d" % (nm, c))
+                nc.vector.tensor_copy(g[:], rows[:].indirect(offsets[:, c * CH // 16 : (c + 1) * CH // 16]))
+                got.append(g)
+            for c in range(CHUNKS):
+                for h in range(HALVES):
+                    t = keep.tile([P, CH], F32, name="%s_prod%d%d" % (nm, c, h))
+                    nc.vector.tensor_tensor(t[:], y[c, h][:], got[c][:], MULT)
+                    prods[nm, c, h] = t
+
+        for c in range(CHUNKS):
+            for h in range(HALVES):
+                r = keep.tile([P, CH], F32, name="res%d%d" % (c, h))
+                nc.vector.tensor_tensor(
+                    r[:], prods["cos", c, h][:], prods["sin", c, 1 - h][:], SUB if h == 0 else ADD
+                )
+                nc.sync.dma_start(out=out[h * P : (h + 1) * P, c * CH : (c + 1) * CH], in_=r[:])

@@ -29,23 +29,23 @@ def tile_picked_zrope_none_p_kernel(tc, x_words, x_scales, w1, ct, st, offs, out
         keep = ctx.enter_context(tc.tile_pool(name="keep", bufs=1))
         psum = ctx.enter_context(tc.psum_pool(name="psum", bufs=1))
 
-        offsets = keep.tile([P, S // 16], U16, name="offsets")
-        nc.sync.dma_start(offsets[:], offs)
-
         scale_rows = keep.tile([P, T], U8, name="scale_rows", align_bytes=64)
         x_planes = keep.tile([P, S], U8, name="x_planes", align_bytes=64)
         nc.vector.memset(scale_rows[:].bitcast(I32), 0)
         nc.vector.memset(x_planes[:].bitcast(I32), 0)
-        nc.scalar.dma_start(
-            out=scale_rows[0:P:4, :].bitcast(I32),
-            in_=x_scales.rearrange("o q c -> (o q) c").bitcast(I32),
-        )
 
         w_raw = keep.tile([P, PASSES, PACK, N], F32, name="w_raw")
         nc.sync.dma_start(
             out=w_raw[:].rearrange("p o j n -> p o (j n)"),
             in_=w1.rearrange("(o p j) n -> p o (j n)", o=PASSES, j=PACK),
         )
+        nc.sync.dma_start(
+            out=scale_rows[0:P:4, :].bitcast(I32),
+            in_=x_scales.rearrange("o q c -> (o q) c").bitcast(I32),
+        )
+        offsets = keep.tile([P, S // 16], U16, name="offsets")
+        nc.sync.dma_start(offsets[:], offs)
+
         words = []
         for o in range(PASSES):
             t = keep.tile([P, T], U32, name="words%d" % o, align_bytes=64)
@@ -65,7 +65,7 @@ def tile_picked_zrope_none_p_kernel(tc, x_words, x_scales, w1, ct, st, offs, out
             for q in range(4):
                 src = 64 * o + 16 * q
                 dst = 32 * q + 4 * o
-                nc.gpsimd.dma_start(
+                (nc.scalar if o == 0 else nc.gpsimd).dma_start(
                     out=x_planes[dst : dst + 4, :].bitcast(I32),
                     in_=picked_rows[src : src + 13 : 4, :].bitcast(I32),
                 )
@@ -104,23 +104,32 @@ def tile_picked_zrope_none_p_kernel(tc, x_words, x_scales, w1, ct, st, offs, out
                         stop=(o == PASSES - 1),
                     )
 
-        prods = {}
-        for nm, rows in (("cos", cos_rows), ("sin", sin_rows)):
-            got = []
-            for c in range(CHUNKS):
-                g = keep.tile([P, CH], F32, name="%s_picked%d" % (nm, c))
-                nc.vector.tensor_copy(g[:], rows[:].indirect(offsets[:, c * CH // 16 : (c + 1) * CH // 16]))
-                got.append(g)
-            for c in range(CHUNKS):
-                for h in range(HALVES):
-                    t = keep.tile([P, CH], F32, name="%s_prod%d%d" % (nm, c, h))
-                    nc.vector.tensor_tensor(t[:], y[c, h][:], got[c][:], MULT)
-                    prods[nm, c, h] = t
+        def pick(nm, rows, c, tag):
+            g = keep.tile([P, CH], F32, name="%s_picked%d" % (nm, c), tag=tag)
+            nc.vector.tensor_copy(g[:], rows[:].indirect(offsets[:, c * CH // 16 : (c + 1) * CH // 16]))
+            return g
 
+        def times(nm, g, c, h):
+            t = keep.tile([P, CH], F32, name="%s_prod%d%d" % (nm, c, h))
+            nc.vector.tensor_tensor(t[:], y[c, h][:], g[:], MULT)
+            return t
+
+        cos_picked = [pick("cos", cos_rows, c, "angle%d" % c) for c in range(CHUNKS)]
+        cos_prod = {(c, h): times("cos", cos_picked[c], c, h) for c in range(CHUNKS) for h in range(HALVES)}
+        sin_picked = [pick("sin", sin_rows, c, "angle%d" % (CHUNKS - 1 - c)) for c in range(CHUNKS)]
         for c in range(CHUNKS):
-            for h in range(HALVES):
-                r = keep.tile([P, CH], F32, name="res%d%d" % (c, h))
-                nc.vector.tensor_tensor(
-                    r[:], prods["cos", c, h][:], prods["sin", c, 1 - h][:], SUB if h == 0 else ADD
-                )
-                nc.sync.dma_start(out=out[h * P : (h + 1) * P, c * CH : (c + 1) * CH], in_=r[:])
+            sin_prod = [times("sin", sin_picked[c], c, h) for h in range(HALVES)]
+            for h in (1, 0):
+                pieces = 2 if (c, h) == (CHUNKS - 1, 0) else 1
+                w = CH // pieces
+                for i in range(pieces):
+                    r = keep.tile([P, w], F32, name="res%d%d%d" % (c, h, i))
+                    nc.vector.tensor_tensor(
+                        r[:],
+                        cos_prod[c, h][:, i * w : (i + 1) * w],
+                        sin_prod[1 - h][:, i * w : (i + 1) * w],
+                        SUB if h == 0 else ADD,
+                    )
+                    nc.sync.dma_start(
+                        out=out[h * P : (h + 1) * P, c * CH + i * w : c * CH + (i + 1) * w], in_=r[:]
+                    )

@@ -29,10 +29,11 @@ def tile_picked_zrope_none_p_kernel(tc, x_words, x_scales, w1, ct, st, offs, out
         keep = ctx.enter_context(tc.tile_pool(name="keep", bufs=1))
         psum = ctx.enter_context(tc.psum_pool(name="psum", bufs=1))
 
-        scale_rows = keep.tile([P, T], U8, name="scale_rows", align_bytes=64)
-        x_planes = keep.tile([P, S], U8, name="x_planes", align_bytes=64)
+        scale_rows = keep.tile([P, T], U8, name="scale_rows", tag="early_a", align_bytes=64)
+        x_planes = [keep.tile([P, S], U8, name="x_plane%d" % o, align_bytes=64) for o in range(PASSES)]
         nc.vector.memset(scale_rows[:].bitcast(I32), 0)
-        nc.vector.memset(x_planes[:].bitcast(I32), 0)
+        for plane in x_planes:
+            nc.vector.memset(plane[:].bitcast(I32), 0)
 
         w_raw = keep.tile([P, PASSES, PACK, N], F32, name="w_raw")
         nc.sync.dma_start(
@@ -54,23 +55,11 @@ def tile_picked_zrope_none_p_kernel(tc, x_words, x_scales, w1, ct, st, offs, out
                 in_=x_words[o].rearrange("p c r -> p (c r)").bitcast(I32),
             )
             words.append(t)
-        cos_rows = keep.tile([P, T], F32, name="cos_rows", align_bytes=64)
-        nc.sync.dma_start(out=cos_rows[:], in_=ct[0:P, :])
-        sin_rows = keep.tile([P, T], F32, name="sin_rows", align_bytes=64)
-        nc.sync.dma_start(out=sin_rows[:], in_=st[0:P, :])
 
         picked_rows = keep.tile([P, S], U8, name="picked_rows", align_bytes=64)
         nc.vector.tensor_copy(picked_rows[:], scale_rows[:].indirect(offsets[:]))
-        for o in range(PASSES):
-            for q in range(4):
-                src = 64 * o + 16 * q
-                dst = 32 * q + 4 * o
-                (nc.scalar if o == 0 else nc.gpsimd).dma_start(
-                    out=x_planes[dst : dst + 4, :].bitcast(I32),
-                    in_=picked_rows[src : src + 13 : 4, :].bitcast(I32),
-                )
 
-        w_grouped = keep.tile([P, PASSES, N, PACK], BF16, name="w_grouped", align_bytes=64)
+        w_grouped = keep.tile([P, PASSES, N, PACK], BF16, name="w_grouped", tag="early_b", align_bytes=64)
         for o in range(PASSES):
             nc.scalar.copy(out=w_grouped[:, o], in_=w_raw[:, o].rearrange("p j n -> p n j"))
         w_codes = keep.tile([P, PASSES * N], U32, name="w_codes", align_bytes=64)
@@ -81,6 +70,22 @@ def tile_picked_zrope_none_p_kernel(tc, x_words, x_scales, w1, ct, st, offs, out
             in_=w_grouped[:].rearrange("p o n j -> p (o n j)"),
         )
 
+        def move(o, j):
+            nc.sync.dma_start(
+                out=x_planes[o][4 * o + j : P : 32, :].bitcast(I32),
+                in_=picked_rows[64 * o + 4 * j : 64 * (o + 1) : 16, :].bitcast(I32),
+            )
+
+        moves = [(o, j) for o in range(PASSES) for j in range(4)]
+        for o, j in moves[:6]:
+            move(o, j)
+        cos_rows = keep.tile([P, T], F32, name="cos_rows", tag="early_a", align_bytes=64)
+        nc.sync.dma_start(out=cos_rows[:], in_=ct[0:P, :])
+        for o, j in moves[6:]:
+            move(o, j)
+        sin_rows = keep.tile([P, T], F32, name="sin_rows", tag="early_b", align_bytes=64)
+        nc.sync.dma_start(out=sin_rows[:], in_=st[0:P, :])
+
         picked = []
         for o in range(PASSES):
             t = keep.tile([P, S], U32, name="picked%d" % o, align_bytes=64)
@@ -89,17 +94,19 @@ def tile_picked_zrope_none_p_kernel(tc, x_words, x_scales, w1, ct, st, offs, out
 
         y = {}
         for c in range(CHUNKS):
-            cols = slice(c * CH, (c + 1) * CH)
             for h in range(HALVES):
                 y[c, h] = psum.tile([P, CH], F32, name="y%d%d" % (c, h))
-                for o in range(PASSES):
+        for o in range(PASSES):
+            for c in range(CHUNKS):
+                cols = slice(c * CH, (c + 1) * CH)
+                for h in range(HALVES):
                     wc = slice(o * N + h * P, o * N + (h + 1) * P)
                     nc.tensor.matmul_mx(
                         out=y[c, h][:],
                         lhsT=w_codes[:, wc].bitcast(FP8X4),
                         lhsT_scale=w_planes[:, wc],
                         rhs=picked[o][:, cols].bitcast(FP8X4),
-                        rhs_scale=x_planes[4 * o :, cols],
+                        rhs_scale=x_planes[o][4 * o :, cols],
                         start=(o == 0),
                         stop=(o == PASSES - 1),
                     )

@@ -1,6 +1,7 @@
 from contextlib import ExitStack
 
 import concourse.mybir as mybir
+from concourse.masks import make_identity
 
 K, T, S, N = 1024, 4096, 1024, 256
 FLOPS = 2 * K * S * N
@@ -95,7 +96,7 @@ def tile_picked_zrope_none_p_kernel(tc, x_words, x_scales, w1, ct, st, offs, out
         y = {}
         for c in range(CHUNKS):
             for h in range(HALVES):
-                y[c, h] = psum.tile([P, CH], F32, name="y%d%d" % (c, h))
+                y[c, h] = psum.tile([P, CH], F32, name="y%d%d" % (c, h), tag="y%d%d" % (c, h))
         for o in range(PASSES):
             for c in range(CHUNKS):
                 cols = slice(c * CH, (c + 1) * CH)
@@ -116,27 +117,60 @@ def tile_picked_zrope_none_p_kernel(tc, x_words, x_scales, w1, ct, st, offs, out
             nc.vector.tensor_copy(g[:], rows[:].indirect(offsets[:, c * CH // 16 : (c + 1) * CH // 16]))
             return g
 
-        def times(nm, g, c, h):
-            t = keep.tile([P, CH], F32, name="%s_prod%d%d" % (nm, c, h))
-            nc.vector.tensor_tensor(t[:], y[c, h][:], g[:], MULT)
+        identity = keep.tile([P, P], F32, name="identity")
+        make_identity(nc, identity[:])
+
+        def hold(h):
+            t = keep.tile([P, CH], F32, name="y_held%d" % h)
+            nc.scalar.copy(out=t[:], in_=y[0, h][:])
             return t
 
-        cos_picked = [pick("cos", cos_rows, c, "angle%d" % c) for c in range(CHUNKS)]
-        cos_prod = {(c, h): times("cos", cos_picked[c], c, h) for c in range(CHUNKS) for h in range(HALVES)}
-        sin_picked = [pick("sin", sin_rows, c, "angle%d" % (CHUNKS - 1 - c)) for c in range(CHUNKS)]
-        for c in range(CHUNKS):
-            sin_prod = [times("sin", sin_picked[c], c, h) for h in range(HALVES)]
-            for h in (1, 0):
-                pieces = 2 if (c, h) == (CHUNKS - 1, 0) else 1
-                w = CH // pieces
-                for i in range(pieces):
-                    r = keep.tile([P, w], F32, name="res%d%d%d" % (c, h, i))
-                    nc.vector.tensor_tensor(
-                        r[:],
-                        cos_prod[c, h][:, i * w : (i + 1) * w],
-                        sin_prod[1 - h][:, i * w : (i + 1) * w],
-                        SUB if h == 0 else ADD,
-                    )
-                    nc.sync.dma_start(
-                        out=out[h * P : (h + 1) * P, c * CH + i * w : c * CH + (i + 1) * w], in_=r[:]
-                    )
+        def times(eng, nm, factor, g):
+            t = keep.tile([P, CH], F32, name=nm)
+            eng.tensor_tensor(t[:], factor[:], g[:], MULT)
+            return t
+
+        def turn(nm, src, tag):
+            dst = psum.tile([P, CH], F32, name=nm, tag=tag)
+            for b in range(CH // P):
+                nc.tensor.transpose(dst[:, b * P : (b + 1) * P], src[:, b * P : (b + 1) * P], identity[:])
+            return dst
+
+        def stage(nm, src):
+            dst = keep.tile([P, CH], F32, name=nm)
+            nc.scalar.copy(out=dst[:], in_=src[:])
+            return dst
+
+        def finish(eng, queue, c, h, cos_term, sin_term, lo, hi):
+            r = keep.tile([P, hi - lo], F32, name="res%d%d%d" % (c, h, lo))
+            eng.tensor_tensor(r[:], cos_term[:, lo:hi], sin_term[:, lo:hi], SUB if h == 0 else ADD)
+            queue.dma_start(out=out[h * P : (h + 1) * P, c * CH + lo : c * CH + hi], in_=r[:])
+
+        cos0 = pick("cos", cos_rows, 0, "angle0")
+        cos1 = pick("cos", cos_rows, 1, "angle1")
+        a01 = times(nc.gpsimd, "a01", hold(1), cos0)
+        a00 = times(nc.vector, "a00", y[0, 0], cos0)
+        a11 = times(nc.vector, "a11", y[1, 1], cos1)
+        a10 = times(nc.vector, "a10", y[1, 0], cos1)
+        y00_held = hold(0)
+        a00_turned = turn("a00_turned", a00, "turn0")
+        a11_turned = turn("a11_turned", a11, "turn1")
+        a10_turned = turn("a10_turned", a10, "y00")
+        a00 = turn("a00_parked", stage("a00_staged", a00_turned), "park0")
+        a11 = turn("a11_parked", stage("a11_staged", a11_turned), "park1")
+        a10 = turn("a10_parked", stage("a10_staged", a10_turned), "turn0")
+
+        sin0 = pick("sin", sin_rows, 0, "angle1")
+        sin1 = pick("sin", sin_rows, 1, "angle0")
+        H = CH // 2
+        t00 = times(nc.gpsimd, "t00", y00_held, sin0)
+        finish(nc.gpsimd, nc.scalar, 0, 1, a01, t00, 0, H)
+        finish(nc.gpsimd, nc.scalar, 0, 1, a01, t00, H, CH)
+        t01 = times(nc.vector, "t01", y[0, 1], sin0)
+        t10 = times(nc.vector, "t10", y[1, 0], sin1)
+        finish(nc.vector, nc.sync, 0, 0, a00, t01, 0, CH)
+        finish(nc.vector, nc.sync, 1, 1, a11, t10, 0, H)
+        t11 = times(nc.vector, "t11", y[1, 1], sin1)
+        finish(nc.vector, nc.sync, 1, 1, a11, t10, H, CH)
+        finish(nc.vector, nc.sync, 1, 0, a10, t11, 0, H)
+        finish(nc.vector, nc.sync, 1, 0, a10, t11, H, CH)

@@ -30,23 +30,23 @@ def tile_picked_zrope_none_p_kernel(tc, x_words, x_scales, w1, ct, st, offs, out
         keep = ctx.enter_context(tc.tile_pool(name="keep", bufs=1))
         psum = ctx.enter_context(tc.psum_pool(name="psum", bufs=1))
 
-        scale_rows = keep.tile([P, T], U8, name="scale_rows", tag="early_a", align_bytes=64)
-        x_planes = [keep.tile([P, S], U8, name="x_plane%d" % o, align_bytes=64) for o in range(PASSES)]
-        nc.vector.memset(scale_rows[:].bitcast(I32), 0)
-        for plane in x_planes:
-            nc.vector.memset(plane[:].bitcast(I32), 0)
+        scale_rows = keep.tile([P, PASSES, T], U8, name="scale_rows", tag="early_a", align_bytes=64)
+        x_plane = keep.tile([P, PASSES, S], U8, name="x_plane", align_bytes=64)
+        nc.vector.memset(scale_rows[:, 0, :].bitcast(I32), 0)
+        nc.gpsimd.memset(scale_rows[:, 1, :].bitcast(I32), 0)
+        nc.vector.memset(x_plane[:].bitcast(I32), 0)
 
         w_raw = keep.tile([P, PASSES, PACK, N], F32, name="w_raw")
         nc.sync.dma_start(
             out=w_raw[:].rearrange("p o j n -> p o (j n)"),
             in_=w1.rearrange("(o p j) n -> p o (j n)", o=PASSES, j=PACK),
         )
-        nc.sync.dma_start(
-            out=scale_rows[0:P:4, :].bitcast(I32),
-            in_=x_scales.rearrange("o q c -> (o q) c").bitcast(I32),
-        )
         offsets = keep.tile([P, S // 16], U16, name="offsets")
         nc.sync.dma_start(offsets[:], offs)
+        nc.sync.dma_start(
+            out=scale_rows[0:P:8].bitcast(I32),
+            in_=x_scales.rearrange("o q c -> q o c").bitcast(I32),
+        )
 
         words = []
         for o in range(PASSES):
@@ -57,8 +57,9 @@ def tile_picked_zrope_none_p_kernel(tc, x_words, x_scales, w1, ct, st, offs, out
             )
             words.append(t)
 
-        picked_rows = keep.tile([P, S], U8, name="picked_rows", align_bytes=64)
-        nc.vector.tensor_copy(picked_rows[:], scale_rows[:].indirect(offsets[:]))
+        picked_rows = keep.tile([P, PASSES, S], U8, name="picked_rows", align_bytes=64)
+        for o in range(PASSES):
+            nc.vector.tensor_copy(picked_rows[:, o, :], scale_rows[:, o, :].indirect(offsets[:]))
 
         w_grouped = keep.tile([P, PASSES, N, PACK], BF16, name="w_grouped", tag="early_b", align_bytes=64)
         for o in range(PASSES):
@@ -71,19 +72,13 @@ def tile_picked_zrope_none_p_kernel(tc, x_words, x_scales, w1, ct, st, offs, out
             in_=w_grouped[:].rearrange("p o n j -> p (o n j)"),
         )
 
-        def move(o, j):
+        for j in range(4):
             nc.sync.dma_start(
-                out=x_planes[o][4 * o + j : P : 32, :].bitcast(I32),
-                in_=picked_rows[64 * o + 4 * j : 64 * (o + 1) : 16, :].bitcast(I32),
+                out=x_plane[j:P:32].rearrange("p o s -> p (o s)").bitcast(I32),
+                in_=picked_rows[8 * j : P : 32].rearrange("p o s -> p (o s)").bitcast(I32),
             )
-
-        moves = [(o, j) for o in range(PASSES) for j in range(4)]
-        for o, j in moves[:6]:
-            move(o, j)
         cos_rows = keep.tile([P, T], F32, name="cos_rows", tag="early_a", align_bytes=64)
         nc.sync.dma_start(out=cos_rows[:], in_=ct[0:P, :])
-        for o, j in moves[6:]:
-            move(o, j)
         sin_rows = keep.tile([P, T], F32, name="sin_rows", tag="early_b", align_bytes=64)
         nc.sync.dma_start(out=sin_rows[:], in_=st[0:P, :])
 
@@ -93,24 +88,45 @@ def tile_picked_zrope_none_p_kernel(tc, x_words, x_scales, w1, ct, st, offs, out
             nc.vector.tensor_copy(t[:], words[o][:].indirect(offsets[:]))
             picked.append(t)
 
-        y = {}
-        for c in range(CHUNKS):
-            for h in range(HALVES):
-                y[c, h] = psum.tile([P, CH], F32, name="y%d%d" % (c, h), tag="y%d%d" % (c, h))
-        for o in range(PASSES):
-            for c in range(CHUNKS):
-                cols = slice(c * CH, (c + 1) * CH)
-                for h in range(HALVES):
-                    wc = slice(o * N + h * P, o * N + (h + 1) * P)
-                    nc.tensor.matmul_mx(
-                        out=y[c, h][:],
-                        lhsT=w_codes[:, wc].bitcast(FP8X4),
-                        lhsT_scale=w_planes[:, wc],
-                        rhs=picked[o][:, cols].bitcast(FP8X4),
-                        rhs_scale=x_planes[o][4 * o :, cols],
-                        start=(o == 0),
-                        stop=(o == PASSES - 1),
-                    )
+        H = CH // 2
+
+        def mx(dst, o, cols, wc, tokens_stationary):
+            x_side = (picked[o][:, cols].bitcast(FP8X4), x_plane[:, o, cols])
+            w_side = (w_codes[:, wc].bitcast(FP8X4), w_planes[:, wc])
+            still, moving = (x_side, w_side) if tokens_stationary else (w_side, x_side)
+            nc.tensor.matmul_mx(
+                out=dst,
+                lhsT=still[0],
+                lhsT_scale=still[1],
+                rhs=moving[0],
+                rhs_scale=moving[1],
+                start=(o == 0),
+                stop=(o == PASSES - 1),
+            )
+
+        def w_cols(o, h):
+            return slice(o * N + h * P, o * N + (h + 1) * P)
+
+        y_b = [psum.tile([P, CH], F32, name="y_b%d" % h, tag="y_b%d" % h) for h in range(HALVES)]
+        for h in range(HALVES):
+            mx(y_b[h][:], 0, slice(CH, S), w_cols(0, h), False)
+        y_a = psum.tile([P, HALVES, H], F32, name="y_a", tag="y_a")
+        for h in range(HALVES):
+            for o in range(PASSES):
+                mx(y_a[:, h, :], o, slice(H, CH), w_cols(o, h), False)
+        held_a = keep.tile([P, HALVES, H], F32, name="held_a")
+        nc.scalar.copy(out=held_a[:], in_=y_a[:])
+        yt_bank = psum.tile([P, 2, N], F32, name="yt_bank", tag="sum0")
+        for i in range(2):
+            for o in range(PASSES):
+                mx(yt_bank[:, i, :], o, slice(i * P, (i + 1) * P), slice(o * N, (o + 1) * N), True)
+        yt = []
+        for h in range(HALVES):
+            t = keep.tile([P, 2, P], F32, name="yt%d" % h, tag="yt%d" % h)
+            nc.scalar.copy(out=t[:], in_=yt_bank[:, :, h * P : (h + 1) * P])
+            yt.append(t)
+        for h in range(HALVES):
+            mx(y_b[h][:], 1, slice(CH, S), w_cols(1, h), False)
 
         def pick(nm, rows, c, tag):
             g = keep.tile([P, CH], F32, name="%s_picked%d" % (nm, c), tag=tag)
@@ -120,57 +136,97 @@ def tile_picked_zrope_none_p_kernel(tc, x_words, x_scales, w1, ct, st, offs, out
         identity = keep.tile([P, P], F32, name="identity")
         make_identity(nc, identity[:])
 
-        def hold(h):
-            t = keep.tile([P, CH], F32, name="y_held%d" % h)
-            nc.scalar.copy(out=t[:], in_=y[0, h][:])
-            return t
+        def for_both(ap):
+            return ap.unsqueeze(1).to_broadcast([P, HALVES, ap.shape[1]])
 
-        def times(eng, nm, factor, g):
-            t = keep.tile([P, CH], F32, name=nm)
-            eng.tensor_tensor(t[:], factor[:], g[:], MULT)
-            return t
-
-        def turn(nm, src, tag):
-            dst = psum.tile([P, CH], F32, name=nm, tag=tag)
-            for b in range(CH // P):
+        def turn(dst, src, blocks):
+            for b in range(blocks):
                 nc.tensor.transpose(dst[:, b * P : (b + 1) * P], src[:, b * P : (b + 1) * P], identity[:])
-            return dst
 
-        def stage(nm, src):
-            dst = keep.tile([P, CH], F32, name=nm)
-            nc.scalar.copy(out=dst[:], in_=src[:])
-            return dst
+        def turned_term(nm, h, angles, swap):
+            t = keep.tile([P, 2, P], F32, name="%s%d" % (nm, h), tag="%s%d" % (nm, h))
+            nc.vector.scalar_tensor_tensor(
+                t[:],
+                yt[h ^ swap][:],
+                -1.0 if swap and h == 0 else 1.0,
+                angles.rearrange("p (i f) -> p i f", i=2),
+                MULT,
+                MULT,
+            )
+            for i in range(2):
+                nc.tensor.matmul(
+                    sums[h][:, i * P : (i + 1) * P],
+                    t[:, i, :],
+                    identity[:],
+                    is_transpose=True,
+                    start=(not swap and i == 0),
+                    stop=(swap == 1 and i == 1),
+                )
 
-        def finish(eng, queue, c, h, cos_term, sin_term, lo, hi):
-            r = keep.tile([P, hi - lo], F32, name="res%d%d%d" % (c, h, lo))
-            eng.tensor_tensor(r[:], cos_term[:, lo:hi], sin_term[:, lo:hi], SUB if h == 0 else ADD)
-            queue.dma_start(out=out[h * P : (h + 1) * P, c * CH + lo : c * CH + hi], in_=r[:])
+        def park(nm, factor, angles, turn_tag):
+            width = factor.shape[1]
+            term = keep.tile([P, width], F32, name=nm)
+            nc.vector.tensor_tensor(term[:], factor, angles, MULT)
+            turned = psum.tile([P, width], F32, name=nm + "_turned", tag=turn_tag)
+            turn(turned, term, width // P)
+            staged = keep.tile([P, width], F32, name=nm + "_staged")
+            nc.scalar.copy(out=staged[:], in_=turned[:])
+            return staged
 
-        cos0 = pick("cos", cos_rows, 0, "angle0")
-        cos1 = pick("cos", cos_rows, 1, "angle1")
-        a01 = times(nc.gpsimd, "a01", hold(1), cos0)
-        a00 = times(nc.vector, "a00", y[0, 0], cos0)
-        a11 = times(nc.vector, "a11", y[1, 1], cos1)
-        a10 = times(nc.vector, "a10", y[1, 0], cos1)
-        y00_held = hold(0)
-        a00_turned = turn("a00_turned", a00, "turn0")
-        a11_turned = turn("a11_turned", a11, "turn1")
-        a10_turned = turn("a10_turned", a10, "y00")
-        a00 = turn("a00_parked", stage("a00_staged", a00_turned), "park0")
-        a11 = turn("a11_parked", stage("a11_staged", a11_turned), "park1")
-        a10 = turn("a10_parked", stage("a10_staged", a10_turned), "turn0")
+        def park_back(nm, staged, tag):
+            width = staged.shape[1]
+            parked = psum.tile([P, width], F32, name=nm, tag=tag)
+            turn(parked, staged, width // P)
+            return parked
 
-        sin0 = pick("sin", sin_rows, 0, "angle1")
-        sin1 = pick("sin", sin_rows, 1, "angle0")
-        H = CH // 2
-        t00 = times(nc.gpsimd, "t00", y00_held, sin0)
-        finish(nc.gpsimd, nc.scalar, 0, 1, a01, t00, 0, H)
-        finish(nc.gpsimd, nc.scalar, 0, 1, a01, t00, H, CH)
-        t01 = times(nc.vector, "t01", y[0, 1], sin0)
-        t10 = times(nc.vector, "t10", y[1, 0], sin1)
-        finish(nc.vector, nc.sync, 0, 0, a00, t01, 0, CH)
-        finish(nc.vector, nc.sync, 1, 1, a11, t10, 0, H)
-        t11 = times(nc.vector, "t11", y[1, 1], sin1)
-        finish(nc.vector, nc.sync, 1, 1, a11, t10, H, CH)
-        finish(nc.vector, nc.sync, 1, 0, a10, t11, 0, H)
-        finish(nc.vector, nc.sync, 1, 0, a10, t11, H, CH)
+        cos = [pick("cos", cos_rows, 0, "cos0"), pick("cos", cos_rows, 1, "cos1")]
+        cos_turned = psum.tile([P, H], F32, name="cos_turned", tag="angle_bank")
+        turn(cos_turned, cos[0], 2)
+        a_a = keep.tile([P, HALVES, H], F32, name="a_a")
+        nc.gpsimd.tensor_tensor(a_a[:], held_a[:], for_both(cos[0][:, H:]), MULT)
+        staged = [park("a%d" % h, y_b[h][:], cos[1][:], tag) for h, tag in ((0, "y_a"), (1, "turn"))]
+        sums = [psum.tile([P, H], F32, name="sum%d" % h, tag="sum%d" % h) for h in range(HALVES)]
+        for h in range(HALVES):
+            turned_term("at", h, cos_turned[:], 0)
+        a0 = park_back("a0_parked", staged[0], "park")
+
+        def finish(eng, h, cos_term, sin_term, lo):
+            r = keep.tile([P, H], F32, name="res%d%d" % (h, lo))
+            eng.tensor_tensor(r[:], cos_term, sin_term, SUB if h == 0 else ADD)
+            nc.sync.dma_start(out=out[h * P : (h + 1) * P, lo : lo + H], in_=r[:])
+
+        joint = keep.tile([P, CH], F32, name="joint")
+
+        sin_a = pick("sin", sin_rows, 0, "cos1")
+        sin_b = pick("sin", sin_rows, 1, "cos0")
+        sin_turned = psum.tile([P, H], F32, name="sin_turned", tag="turn")
+        turn(sin_turned, sin_a, 2)
+        for h in range(HALVES):
+            t = keep.tile([P, H], F32, name="t_a%d" % h, tag="t_a")
+            nc.gpsimd.tensor_tensor(t[:], held_a[:, 1 - h, :], sin_a[:, H:], MULT)
+            if h == 0:
+                finish(nc.gpsimd, h, a_a[:, h, :], t[:], H)
+            else:
+                nc.gpsimd.tensor_tensor(joint[:, :H], a_a[:, h, :], t[:], ADD)
+        for h in range(HALVES):
+            turned_term("tt", h, sin_turned[:], 1)
+            r = keep.tile([P, H], F32, name="res_turned%d" % h)
+            nc.scalar.copy(out=r[:], in_=sums[h][:])
+            nc.scalar.dma_start(out=out[h * P : (h + 1) * P, :H], in_=r[:])
+
+        a1 = park_back("a1_parked", staged[1], "turn")
+
+        def sine_term(h, lo, tag):
+            t = keep.tile([P, H], F32, name="t_b%d%d" % (h, lo), tag=tag)
+            nc.vector.tensor_tensor(t[:], y_b[1 - h][:, lo : lo + H], sin_b[:, lo : lo + H], MULT)
+            return t
+
+        t0_lo = sine_term(0, 0, "yt1")
+        t0_hi = sine_term(0, H, "yt0")
+        finish(nc.vector, 0, a0[:, :H], t0_lo[:], CH)
+        t1_lo = sine_term(1, 0, "tt0")
+        finish(nc.vector, 0, a0[:, H:], t0_hi[:], CH + H)
+        t1_hi = sine_term(1, H, "tt1")
+        nc.vector.tensor_tensor(joint[:, H:], a1[:, :H], t1_lo[:], ADD)
+        nc.sync.dma_start(out=out[P:, H : H + CH], in_=joint[:])
+        finish(nc.vector, 1, a1[:, H:], t1_hi[:], CH + H)

@@ -30,40 +30,44 @@ def tile_picked_zrope_none_p_kernel(tc, x_words, x_scales, w1, ct, st, offs, out
         keep = ctx.enter_context(tc.tile_pool(name="keep", bufs=1))
         psum = ctx.enter_context(tc.psum_pool(name="psum", bufs=1))
 
-        scale_rows = keep.tile([P, PASSES, T], U8, name="scale_rows", tag="early_a", align_bytes=64)
-        x_plane = keep.tile([P, PASSES, S], U8, name="x_plane", align_bytes=64)
-        nc.vector.memset(scale_rows[:, 0, :].bitcast(I32), 0)
-        nc.gpsimd.memset(scale_rows[:, 1, :].bitcast(I32), 0)
-        nc.vector.memset(x_plane[:].bitcast(I32), 0)
+        scale_rows = keep.tile([P, T], U8, name="scale_rows", tag="early_a", align_bytes=64)
+        x_planes = [keep.tile([P, S], U8, name="x_plane%d" % o, align_bytes=64) for o in range(PASSES)]
+        nc.vector.memset(scale_rows[:, : T // 2].bitcast(I32), 0)
+        nc.gpsimd.memset(scale_rows[:, T // 2 :].bitcast(I32), 0)
+        for plane in x_planes:
+            nc.vector.memset(plane[:].bitcast(I32), 0)
 
-        w_raw = keep.tile([P, PASSES, PACK, N], F32, name="w_raw")
-        nc.sync.dma_start(
-            out=w_raw[:].rearrange("p o j n -> p o (j n)"),
-            in_=w1.rearrange("(o p j) n -> p o (j n)", o=PASSES, j=PACK),
-        )
-        offsets = keep.tile([P, S // 16], U16, name="offsets")
-        nc.sync.dma_start(offsets[:], offs)
-        nc.sync.dma_start(
-            out=scale_rows[0:P:8].bitcast(I32),
-            in_=x_scales.rearrange("o q c -> q o c").bitcast(I32),
-        )
+        w_rows = w1.rearrange("(o p j) n -> o p (j n)", o=PASSES, j=PACK)
 
-        words = []
-        for o in range(PASSES):
-            t = keep.tile([P, T], U32, name="words%d" % o, align_bytes=64)
+        def load_w(o):
+            t = keep.tile([P, PACK, N], F32, name="w_raw%d" % o)
+            nc.sync.dma_start(out=t[:].rearrange("p j n -> p (j n)"), in_=w_rows[o])
+            return t
+
+        def load_words(o, tag):
+            t = keep.tile([P, T], U32, name="words%d" % o, tag=tag, align_bytes=64)
             nc.sync.dma_start(
                 out=t[:].bitcast(I32),
                 in_=x_words[o].rearrange("p c r -> p (c r)").bitcast(I32),
             )
-            words.append(t)
+            return t
 
-        picked_rows = keep.tile([P, PASSES, S], U8, name="picked_rows", align_bytes=64)
-        for o in range(PASSES):
-            nc.vector.tensor_copy(picked_rows[:, o, :], scale_rows[:, o, :].indirect(offsets[:]))
+        w_raw = [load_w(0)]
+        offsets = keep.tile([P, S // 16], U16, name="offsets")
+        nc.sync.dma_start(offsets[:], offs)
+        nc.sync.dma_start(
+            out=scale_rows[0:P:4, :].bitcast(I32),
+            in_=x_scales.rearrange("o q c -> (o q) c").bitcast(I32),
+        )
+        w_raw.append(load_w(1))
+        words = [load_words(0, "early_c")]
+
+        picked_rows = keep.tile([P, S], U8, name="picked_rows", align_bytes=64)
+        nc.vector.tensor_copy(picked_rows[:], scale_rows[:].indirect(offsets[:]))
 
         w_grouped = keep.tile([P, PASSES, N, PACK], BF16, name="w_grouped", tag="early_b", align_bytes=64)
         for o in range(PASSES):
-            nc.scalar.copy(out=w_grouped[:, o], in_=w_raw[:, o].rearrange("p j n -> p n j"))
+            nc.scalar.copy(out=w_grouped[:, o], in_=w_raw[o][:].rearrange("p j n -> p n j"))
         w_codes = keep.tile([P, PASSES * N], U32, name="w_codes", align_bytes=64)
         w_planes = keep.tile([P, PASSES * N], U8, name="w_planes", align_bytes=64)
         nc.vector.quantize_mx(
@@ -72,26 +76,33 @@ def tile_picked_zrope_none_p_kernel(tc, x_words, x_scales, w1, ct, st, offs, out
             in_=w_grouped[:].rearrange("p o n j -> p (o n j)"),
         )
 
-        for j in range(4):
+        def move(o, j):
             nc.sync.dma_start(
-                out=x_plane[j:P:32].rearrange("p o s -> p (o s)").bitcast(I32),
-                in_=picked_rows[8 * j : P : 32].rearrange("p o s -> p (o s)").bitcast(I32),
+                out=x_planes[o][4 * o + j : P : 32, :].bitcast(I32),
+                in_=picked_rows[64 * o + 4 * j : 64 * (o + 1) : 16, :].bitcast(I32),
             )
-        cos_rows = keep.tile([P, T], F32, name="cos_rows", tag="early_a", align_bytes=64)
+
+        moves = [(o, j) for o in range(PASSES) for j in range(4)]
+        for o, j in moves[:2]:
+            move(o, j)
+        words.append(load_words(1, "early_a"))
+        for o, j in moves[2:]:
+            move(o, j)
+        cos_rows = keep.tile([P, T], F32, name="cos_rows", tag="early_b", align_bytes=64)
         nc.sync.dma_start(out=cos_rows[:], in_=ct[0:P, :])
-        sin_rows = keep.tile([P, T], F32, name="sin_rows", tag="early_b", align_bytes=64)
-        nc.sync.dma_start(out=sin_rows[:], in_=st[0:P, :])
 
         picked = []
         for o in range(PASSES):
             t = keep.tile([P, S], U32, name="picked%d" % o, align_bytes=64)
             nc.vector.tensor_copy(t[:], words[o][:].indirect(offsets[:]))
             picked.append(t)
+        sin_rows = keep.tile([P, T], F32, name="sin_rows", tag="early_c", align_bytes=64)
+        nc.sync.dma_start(out=sin_rows[:], in_=st[0:P, :])
 
         H = CH // 2
 
         def mx(dst, o, cols, wc, tokens_stationary):
-            x_side = (picked[o][:, cols].bitcast(FP8X4), x_plane[:, o, cols])
+            x_side = (picked[o][:, cols].bitcast(FP8X4), x_planes[o][4 * o :, cols])
             w_side = (w_codes[:, wc].bitcast(FP8X4), w_planes[:, wc])
             still, moving = (x_side, w_side) if tokens_stationary else (w_side, x_side)
             nc.tensor.matmul_mx(
@@ -184,7 +195,9 @@ def tile_picked_zrope_none_p_kernel(tc, x_words, x_scales, w1, ct, st, offs, out
         turn(cos_turned, cos[0], 2)
         a_a = keep.tile([P, HALVES, H], F32, name="a_a")
         nc.gpsimd.tensor_tensor(a_a[:], held_a[:], for_both(cos[0][:, H:]), MULT)
-        staged = [park("a%d" % h, y_b[h][:], cos[1][:], tag) for h, tag in ((0, "y_a"), (1, "turn"))]
+        staged = [park("a0", y_b[0][:], cos[1][:], "y_a"), park("a1", y_b[1][:, :H], cos[1][:, :H], "turn")]
+        a1_hi = keep.tile([P, H], F32, name="a1_hi")
+        nc.vector.tensor_tensor(a1_hi[:], y_b[1][:, H:], cos[1][:, H:], MULT)
         sums = [psum.tile([P, H], F32, name="sum%d" % h, tag="sum%d" % h) for h in range(HALVES)]
         for h in range(HALVES):
             turned_term("at", h, cos_turned[:], 0)
@@ -227,6 +240,6 @@ def tile_picked_zrope_none_p_kernel(tc, x_words, x_scales, w1, ct, st, offs, out
         t1_lo = sine_term(1, 0, "tt0")
         finish(nc.vector, 0, a0[:, H:], t0_hi[:], CH + H)
         t1_hi = sine_term(1, H, "tt1")
-        nc.vector.tensor_tensor(joint[:, H:], a1[:, :H], t1_lo[:], ADD)
+        nc.vector.tensor_tensor(joint[:, H:], a1[:], t1_lo[:], ADD)
         nc.sync.dma_start(out=out[P:, H : H + CH], in_=joint[:])
-        finish(nc.vector, 1, a1[:, H:], t1_hi[:], CH + H)
+        finish(nc.vector, 1, a1_hi[:], t1_hi[:], CH + H)

@@ -118,55 +118,60 @@ def tile_picked_zrope_none_p_kernel(tc, x_words, x_scales, w1, ct, st, offs, out
         def w_cols(o, h):
             return slice(o * N + h * P, o * N + (h + 1) * P)
 
-        y_b = [psum.tile([P, CH], F32, name="y_b%d" % h, tag="y_b%d" % h) for h in range(HALVES)]
+        y_b = [psum.tile([P, CH], F32, name="y_b%d" % h, tag="bank%d" % h) for h in range(HALVES)]
         for h in range(HALVES):
             mx(y_b[h][:], 0, slice(CH, S), w_cols(0, h), False)
-        y_a = psum.tile([P, HALVES, H], F32, name="y_a", tag="y_a")
+        y_a = psum.tile([P, HALVES, H], F32, name="y_a", tag="bank4")
         for h in range(HALVES):
             for o in range(PASSES):
                 mx(y_a[:, h, :], o, slice(H, CH), w_cols(o, h), False)
         held_a = keep.tile([P, HALVES, H], F32, name="held_a")
         nc.scalar.copy(out=held_a[:], in_=y_a[:])
-        yt_bank = psum.tile([P, 2, N], F32, name="yt_bank", tag="sum0")
-        for i in range(2):
-            for o in range(PASSES):
-                mx(yt_bank[:, i, :], o, slice(i * P, (i + 1) * P), slice(o * N, (o + 1) * N), True)
-        yt = []
-        for h in range(HALVES):
-            t = keep.tile([P, 2, P], F32, name="yt%d" % h, tag="yt%d" % h)
-            nc.scalar.copy(out=t[:], in_=yt_bank[:, :, h * P : (h + 1) * P])
-            yt.append(t)
+        yt = {}
+        for q in range(2):
+            yt_bank = psum.tile([P, 2, N], F32, name="yt_bank%d" % q, tag="bank%d" % (2 + q))
+            for i in range(2):
+                lo = q * H + i * P
+                for o in range(PASSES):
+                    mx(yt_bank[:, i, :], o, slice(lo, lo + P), slice(o * N, (o + 1) * N), True)
+            for h in range(HALVES):
+                t = keep.tile([P, 2, P], F32, name="yt%d%d" % (h, q), tag="yt%d%d" % (h, q))
+                nc.scalar.copy(out=t[:], in_=yt_bank[:, :, h * P : (h + 1) * P])
+                yt[h, q] = t
         for h in range(HALVES):
             mx(y_b[h][:], 1, slice(CH, S), w_cols(1, h), False)
+        held_lo = keep.tile([P, H], F32, name="held_lo")
+        nc.scalar.copy(out=held_lo[:], in_=y_b[0][:, :H])
+        held_hi = keep.tile([P, CH], F32, name="held_hi")
+        nc.scalar.copy(out=held_hi[:], in_=y_b[1][:])
 
-        def pick(nm, rows, c, tag):
-            g = keep.tile([P, CH], F32, name="%s_picked%d" % (nm, c), tag=tag)
+        def pick(nm, rows, c):
+            g = keep.tile([P, CH], F32, name="%s_picked%d" % (nm, c), tag="%s%d" % (nm, c))
             nc.vector.tensor_copy(g[:], rows[:].indirect(offsets[:, c * CH // 16 : (c + 1) * CH // 16]))
             return g
 
         identity = keep.tile([P, P], F32, name="identity")
         make_identity(nc, identity[:])
 
-        def for_both(ap):
-            return ap.unsqueeze(1).to_broadcast([P, HALVES, ap.shape[1]])
+        def turn(nm, src, lo, blocks, bank):
+            dst = psum.tile([P, blocks * P], F32, name=nm, tag="bank%d" % bank)
+            for i in range(blocks):
+                nc.tensor.transpose(dst[:, i * P : (i + 1) * P], src[:, lo + i * P : lo + (i + 1) * P], identity[:])
+            return dst
 
-        def turn(dst, src, blocks):
-            for b in range(blocks):
-                nc.tensor.transpose(dst[:, b * P : (b + 1) * P], src[:, b * P : (b + 1) * P], identity[:])
-
-        def turned_term(nm, h, angles, swap):
-            t = keep.tile([P, 2, P], F32, name="%s%d" % (nm, h), tag="%s%d" % (nm, h))
+        def turned_term(nm, h, q, angles, swap):
+            t = keep.tile([P, 2, P], F32, name="%s%d%d" % (nm, h, q), tag="%s%d%d" % (nm, h, q))
             nc.vector.scalar_tensor_tensor(
                 t[:],
-                yt[h ^ swap][:],
+                yt[h ^ swap, q][:],
                 -1.0 if swap and h == 0 else 1.0,
-                angles.rearrange("p (i f) -> p i f", i=2),
+                angles[:].rearrange("p (i f) -> p i f", i=2),
                 MULT,
                 MULT,
             )
             for i in range(2):
                 nc.tensor.matmul(
-                    sums[h][:, i * P : (i + 1) * P],
+                    sums[h, q][:, i * P : (i + 1) * P],
                     t[:, i, :],
                     identity[:],
                     is_transpose=True,
@@ -174,72 +179,49 @@ def tile_picked_zrope_none_p_kernel(tc, x_words, x_scales, w1, ct, st, offs, out
                     stop=(swap == 1 and i == 1),
                 )
 
-        def park(nm, factor, angles, turn_tag):
-            width = factor.shape[1]
-            term = keep.tile([P, width], F32, name=nm)
-            nc.vector.tensor_tensor(term[:], factor, angles, MULT)
-            turned = psum.tile([P, width], F32, name=nm + "_turned", tag=turn_tag)
-            turn(turned, term, width // P)
-            staged = keep.tile([P, width], F32, name=nm + "_staged")
-            nc.scalar.copy(out=staged[:], in_=turned[:])
-            return staged
+        def product(eng, nm, factor, angles, tag):
+            t = keep.tile([P, H], F32, name=nm, tag=tag)
+            eng.tensor_tensor(t[:], factor, angles, MULT)
+            return t
 
-        def park_back(nm, staged, tag):
-            width = staged.shape[1]
-            parked = psum.tile([P, width], F32, name=nm, tag=tag)
-            turn(parked, staged, width // P)
-            return parked
+        turned_pieces = ((0, 0), (1, 0), (1, 1))
+        cos = [pick("cos", cos_rows, c) for c in range(CHUNKS)]
+        cos_turned = [turn("cos_turned%d" % q, cos[0], q * H, 2, 5 + q) for q in range(2)]
+        a_g0 = product(nc.gpsimd, "a_g0", held_a[:, 0, :], cos[0][:, H:], "a_g0")
+        a_g1 = product(nc.gpsimd, "a_g1", held_lo[:], cos[1][:, :H], "a_g1")
+        a_last = product(nc.gpsimd, "a_last", held_hi[:, H:], cos[1][:, H:], "a_last")
+        to_park = keep.tile([P, CH], F32, name="to_park")
+        nc.vector.tensor_tensor(to_park[:, :H], y_b[0][:, H:], cos[1][:, H:], MULT)
+        nc.vector.tensor_tensor(to_park[:, H:], y_b[1][:, :H], cos[1][:, :H], MULT)
+        park_turned = turn("park_turned", to_park, 0, 4, 7)
+        staged = keep.tile([P, CH], F32, name="staged")
+        nc.scalar.copy(out=staged[:], in_=park_turned[:])
+        sums = {}
+        for bank, (h, q) in enumerate(turned_pieces):
+            sums[h, q] = psum.tile([P, H], F32, name="sum%d%d" % (h, q), tag="bank%d" % (2 + bank))
+            turned_term("at", h, q, cos_turned[q], 0)
+        parked = turn("parked", staged, 0, 4, 7)
 
-        cos = [pick("cos", cos_rows, 0, "cos0"), pick("cos", cos_rows, 1, "cos1")]
-        cos_turned = psum.tile([P, H], F32, name="cos_turned", tag="angle_bank")
-        turn(cos_turned, cos[0], 2)
-        a_a = keep.tile([P, HALVES, H], F32, name="a_a")
-        nc.gpsimd.tensor_tensor(a_a[:], held_a[:], for_both(cos[0][:, H:]), MULT)
-        staged = [park("a0", y_b[0][:], cos[1][:], "y_a"), park("a1", y_b[1][:, :H], cos[1][:, :H], "turn")]
-        a1_hi = keep.tile([P, H], F32, name="a1_hi")
-        nc.vector.tensor_tensor(a1_hi[:], y_b[1][:, H:], cos[1][:, H:], MULT)
-        sums = [psum.tile([P, H], F32, name="sum%d" % h, tag="sum%d" % h) for h in range(HALVES)]
-        for h in range(HALVES):
-            turned_term("at", h, cos_turned[:], 0)
-        a0 = park_back("a0_parked", staged[0], "park")
-
-        def finish(eng, h, cos_term, sin_term, lo):
-            r = keep.tile([P, H], F32, name="res%d%d" % (h, lo))
+        def finish(eng, nm, h, cos_term, sin_term, lo, tag=None):
+            r = keep.tile([P, H], F32, name=nm, tag=tag or nm)
             eng.tensor_tensor(r[:], cos_term, sin_term, SUB if h == 0 else ADD)
             nc.sync.dma_start(out=out[h * P : (h + 1) * P, lo : lo + H], in_=r[:])
 
-        joint = keep.tile([P, CH], F32, name="joint")
+        sin = [pick("sin", sin_rows, c) for c in range(CHUNKS)]
+        sin_turned = [turn("sin_turned%d" % q, sin[0], q * H, 2, 5 + q) for q in range(2)]
+        t_g0 = product(nc.gpsimd, "t_g0", held_a[:, 1, :], sin[0][:, H:], "t_g0")
+        finish(nc.gpsimd, "res_g0", 0, a_g0[:], t_g0[:], H)
+        t_g1 = product(nc.gpsimd, "t_g1", held_hi[:, :H], sin[1][:, :H], "sin0")
+        for h, q in turned_pieces:
+            turned_term("tt", h, q, sin_turned[q], 1)
+            r = keep.tile([P, H], F32, name="res_turned%d%d" % (h, q))
+            nc.scalar.copy(out=r[:], in_=sums[h, q][:])
+            nc.sync.dma_start(out=out[h * P : (h + 1) * P, q * H : (q + 1) * H], in_=r[:])
 
-        sin_a = pick("sin", sin_rows, 0, "cos1")
-        sin_b = pick("sin", sin_rows, 1, "cos0")
-        sin_turned = psum.tile([P, H], F32, name="sin_turned", tag="turn")
-        turn(sin_turned, sin_a, 2)
-        for h in range(HALVES):
-            t = keep.tile([P, H], F32, name="t_a%d" % h, tag="t_a")
-            nc.gpsimd.tensor_tensor(t[:], held_a[:, 1 - h, :], sin_a[:, H:], MULT)
-            if h == 0:
-                finish(nc.gpsimd, h, a_a[:, h, :], t[:], H)
-            else:
-                nc.gpsimd.tensor_tensor(joint[:, :H], a_a[:, h, :], t[:], ADD)
-        for h in range(HALVES):
-            turned_term("tt", h, sin_turned[:], 1)
-            r = keep.tile([P, H], F32, name="res_turned%d" % h)
-            nc.scalar.copy(out=r[:], in_=sums[h][:])
-            nc.scalar.dma_start(out=out[h * P : (h + 1) * P, :H], in_=r[:])
-
-        a1 = park_back("a1_parked", staged[1], "turn")
-
-        def sine_term(h, lo, tag):
-            t = keep.tile([P, H], F32, name="t_b%d%d" % (h, lo), tag=tag)
-            nc.vector.tensor_tensor(t[:], y_b[1 - h][:, lo : lo + H], sin_b[:, lo : lo + H], MULT)
-            return t
-
-        t0_lo = sine_term(0, 0, "yt1")
-        t0_hi = sine_term(0, H, "yt0")
-        finish(nc.vector, 0, a0[:, :H], t0_lo[:], CH)
-        t1_lo = sine_term(1, 0, "tt0")
-        finish(nc.vector, 0, a0[:, H:], t0_hi[:], CH + H)
-        t1_hi = sine_term(1, H, "tt1")
-        nc.vector.tensor_tensor(joint[:, H:], a1[:], t1_lo[:], ADD)
-        nc.sync.dma_start(out=out[P:, H : H + CH], in_=joint[:])
-        finish(nc.vector, 1, a1_hi[:], t1_hi[:], CH + H)
+        t_b = product(nc.vector, "t_b", y_b[1][:, H:], sin[1][:, H:], "yt00")
+        t_a = product(nc.vector, "t_a", y_b[0][:, :H], sin[1][:, :H], "yt01")
+        finish(nc.vector, "res_b", 0, parked[:, :H], t_b[:], CH + H)
+        finish(nc.gpsimd, "res_g1", 0, a_g1[:], t_g1[:], CH, "tt11")
+        t_c = product(nc.vector, "t_c", y_b[0][:, H:], sin[1][:, H:], "tt00")
+        finish(nc.vector, "res_a", 1, parked[:, H:], t_a[:], CH)
+        finish(nc.vector, "res_c", 1, a_last[:], t_c[:], CH + H)

@@ -221,7 +221,7 @@ def tile_picked_zrope_none_p_kernel(tc, x_words, x_scales, w1, ct, st, offs, out
         t_b = product(nc.vector, "t_b", y_b[1][:, H:], sin[1][:, H:], "yt00")
         t_a = product(nc.vector, "t_a", y_b[0][:, :H], sin[1][:, :H], "yt01")
         finish(nc.vector, "res_b", 0, parked[:, :H], t_b[:], CH + H)
-        finish(nc.gpsimd, "res_g1", 0, a_g1[:], t_g1[:], CH, "tt11")
         t_c = product(nc.vector, "t_c", y_b[0][:, H:], sin[1][:, H:], "tt00")
         finish(nc.vector, "res_a", 1, parked[:, H:], t_a[:], CH)
         finish(nc.vector, "res_c", 1, a_last[:], t_c[:], CH + H)
+        finish(nc.vector, "res_g1", 0, a_g1[:], t_g1[:], CH, "tt11")

@@ -190,17 +190,16 @@ def tile_picked_zrope_none_p_kernel(tc, x_words, x_scales, w1, ct, st, offs, out
         a_g0 = product(nc.gpsimd, "a_g0", held_a[:, 0, :], cos[0][:, H:], "a_g0")
         a_g1 = product(nc.gpsimd, "a_g1", held_lo[:], cos[1][:, :H], "a_g1")
         a_last = product(nc.gpsimd, "a_last", held_hi[:, H:], cos[1][:, H:], "a_last")
-        to_park = keep.tile([P, CH], F32, name="to_park")
-        nc.vector.tensor_tensor(to_park[:, :H], y_b[0][:, H:], cos[1][:, H:], MULT)
-        nc.vector.tensor_tensor(to_park[:, H:], y_b[1][:, :H], cos[1][:, :H], MULT)
-        park_turned = turn("park_turned", to_park, 0, 4, 7)
-        staged = keep.tile([P, CH], F32, name="staged")
+        a_park = product(nc.vector, "a_park", y_b[0][:, H:], cos[1][:, H:], "a_park")
+        a_own = product(nc.vector, "a_own", y_b[1][:, :H], cos[1][:, :H], "a_own")
+        park_turned = turn("park_turned", a_park, 0, 2, 7)
+        staged = keep.tile([P, H], F32, name="staged")
         nc.scalar.copy(out=staged[:], in_=park_turned[:])
         sums = {}
         for bank, (h, q) in enumerate(turned_pieces):
             sums[h, q] = psum.tile([P, H], F32, name="sum%d%d" % (h, q), tag="bank%d" % (2 + bank))
             turned_term("at", h, q, cos_turned[q], 0)
-        parked = turn("parked", staged, 0, 4, 7)
+        parked = turn("parked", staged, 0, 2, 7)
 
         def finish(eng, nm, h, cos_term, sin_term, lo, tag=None):
             r = keep.tile([P, H], F32, name=nm, tag=tag or nm)
@@ -212,16 +211,22 @@ def tile_picked_zrope_none_p_kernel(tc, x_words, x_scales, w1, ct, st, offs, out
         t_g0 = product(nc.gpsimd, "t_g0", held_a[:, 1, :], sin[0][:, H:], "t_g0")
         finish(nc.gpsimd, "res_g0", 0, a_g0[:], t_g0[:], H)
         t_g1 = product(nc.gpsimd, "t_g1", held_hi[:, :H], sin[1][:, :H], "sin0")
-        for h, q in turned_pieces:
+
+        def finish_turned(h, q):
             turned_term("tt", h, q, sin_turned[q], 1)
             r = keep.tile([P, H], F32, name="res_turned%d%d" % (h, q))
             nc.scalar.copy(out=r[:], in_=sums[h, q][:])
             nc.sync.dma_start(out=out[h * P : (h + 1) * P, q * H : (q + 1) * H], in_=r[:])
 
-        t_b = product(nc.vector, "t_b", y_b[1][:, H:], sin[1][:, H:], "yt00")
-        t_a = product(nc.vector, "t_a", y_b[0][:, :H], sin[1][:, :H], "yt01")
-        finish(nc.vector, "res_b", 0, parked[:, :H], t_b[:], CH + H)
-        t_c = product(nc.vector, "t_c", y_b[0][:, H:], sin[1][:, H:], "tt00")
-        finish(nc.vector, "res_a", 1, parked[:, H:], t_a[:], CH)
-        finish(nc.vector, "res_c", 1, a_last[:], t_c[:], CH + H)
-        finish(nc.vector, "res_g1", 0, a_g1[:], t_g1[:], CH, "tt11")
+        finish_turned(0, 0)
+        t_b = product(nc.vector, "t_b", y_b[1][:, H:], sin[1][:, H:], "yt10")
+        finish_turned(1, 0)
+        finish(nc.vector, "res_b", 0, parked[:], t_b[:], CH + H)
+        finish_turned(1, 1)
+        t_a = product(nc.vector, "t_a", y_b[0][:, :H], sin[1][:, :H], "yt00")
+        t_c = product(nc.vector, "t_c", y_b[0][:, H:], sin[1][:, H:], "yt01")
+        finish(nc.vector, "res_g1", 0, a_g1[:], t_g1[:], CH, "tt10")
+        joint = keep.tile([P, CH], F32, name="joint")
+        nc.vector.tensor_tensor(joint[:, :H], a_own[:], t_a[:], ADD)
+        nc.vector.tensor_tensor(joint[:, H:], a_last[:], t_c[:], ADD)
+        nc.sync.dma_start(out=out[P:, CH:], in_=joint[:])

@@ -5,12 +5,13 @@ from concourse.masks import make_identity
 
 K, T, S, N = 1024, 4096, 1024, 256
 FLOPS = 2 * K * S * N
+BYTES = K * T + K * T // 32 + 4 * K * N + 2 * 4 * (N // 2) * T + 2 * 128 * S // 16 + 4 * N * S
 P = 128
 PACK = 4
 PASSES = K // (P * PACK)
 HALVES = N // P
-CH = 512
-CHUNKS = S // CH
+Q = 256
+BLOCKS = Q // P
 
 F32 = mybir.dt.float32
 BF16 = mybir.dt.bfloat16
@@ -22,6 +23,7 @@ FP8X4 = mybir.dt.float8_e4m3fn_x4
 MULT = mybir.AluOpType.mult
 ADD = mybir.AluOpType.add
 SUB = mybir.AluOpType.subtract
+COPY = mybir.ActivationFunctionType.Copy
 
 
 def tile_picked_zrope_none_p_kernel(tc, x_words, x_scales, w1, ct, st, offs, out):
@@ -91,17 +93,20 @@ def tile_picked_zrope_none_p_kernel(tc, x_words, x_scales, w1, ct, st, offs, out
         cos_rows = keep.tile([P, T], F32, name="cos_rows", tag="early_b", align_bytes=64)
         nc.sync.dma_start(out=cos_rows[:], in_=ct[0:P, :])
 
-        picked = []
-        for o in range(PASSES):
-            t = keep.tile([P, S], U32, name="picked%d" % o, align_bytes=64)
-            nc.vector.tensor_copy(t[:], words[o][:].indirect(offsets[:]))
-            picked.append(t)
+        picked = [keep.tile([P, S], U32, name="picked%d" % o, align_bytes=64) for o in range(PASSES)]
+        nc.vector.tensor_copy(picked[0][:], words[0][:].indirect(offsets[:]))
+        for c in range(2):
+            nc.vector.tensor_copy(
+                picked[1][:, c * S // 2 : (c + 1) * S // 2],
+                words[1][:].indirect(offsets[:, c * S // 32 : (c + 1) * S // 32]),
+            )
         sin_rows = keep.tile([P, T], F32, name="sin_rows", tag="early_c", align_bytes=64)
         nc.sync.dma_start(out=sin_rows[:], in_=st[0:P, :])
 
-        H = CH // 2
+        identity = keep.tile([P, P], F32, name="identity")
+        make_identity(nc, identity[:])
 
-        def mx(dst, o, cols, wc, tokens_stationary):
+        def mx(dst, o, cols, wc, tokens_stationary, start, stop):
             x_side = (picked[o][:, cols].bitcast(FP8X4), x_planes[o][4 * o :, cols])
             w_side = (w_codes[:, wc].bitcast(FP8X4), w_planes[:, wc])
             still, moving = (x_side, w_side) if tokens_stationary else (w_side, x_side)
@@ -111,122 +116,111 @@ def tile_picked_zrope_none_p_kernel(tc, x_words, x_scales, w1, ct, st, offs, out
                 lhsT_scale=still[1],
                 rhs=moving[0],
                 rhs_scale=moving[1],
-                start=(o == 0),
-                stop=(o == PASSES - 1),
+                start=start,
+                stop=stop,
             )
 
-        def w_cols(o, h):
-            return slice(o * N + h * P, o * N + (h + 1) * P)
-
-        y_b = [psum.tile([P, CH], F32, name="y_b%d" % h, tag="bank%d" % h) for h in range(HALVES)]
-        for h in range(HALVES):
-            mx(y_b[h][:], 0, slice(CH, S), w_cols(0, h), False)
-        y_a = psum.tile([P, HALVES, H], F32, name="y_a", tag="bank4")
-        for h in range(HALVES):
-            for o in range(PASSES):
-                mx(y_a[:, h, :], o, slice(H, CH), w_cols(o, h), False)
-        held_a = keep.tile([P, HALVES, H], F32, name="held_a")
-        nc.scalar.copy(out=held_a[:], in_=y_a[:])
+        TURNED, PLAIN = (0, 1), (2, 3)
+        y = {q: psum.tile([P, 2, Q], F32, name="y%d" % q, tag="bank%d" % q) for q in range(4)}
+        for o in range(PASSES):
+            for q in range(4):
+                for i in range(2):
+                    first, last = (o == 0 and i == 0), (o == PASSES - 1 and i == 1)
+                    if q in TURNED:
+                        lo = q * Q + i * P
+                        mx(y[q][:, i, :], o, slice(lo, lo + P), slice(o * N, (o + 1) * N), True, first, last)
+                    else:
+                        wc = slice(o * N + i * P, o * N + (i + 1) * P)
+                        mx(y[q][:, i, :], o, slice(q * Q, (q + 1) * Q), wc, False, first, last)
         yt = {}
-        for q in range(2):
-            yt_bank = psum.tile([P, 2, N], F32, name="yt_bank%d" % q, tag="bank%d" % (2 + q))
-            for i in range(2):
-                lo = q * H + i * P
-                for o in range(PASSES):
-                    mx(yt_bank[:, i, :], o, slice(lo, lo + P), slice(o * N, (o + 1) * N), True)
-            for h in range(HALVES):
-                t = keep.tile([P, 2, P], F32, name="yt%d%d" % (h, q), tag="yt%d%d" % (h, q))
-                nc.scalar.copy(out=t[:], in_=yt_bank[:, :, h * P : (h + 1) * P])
-                yt[h, q] = t
-        for h in range(HALVES):
-            mx(y_b[h][:], 1, slice(CH, S), w_cols(1, h), False)
-        held_lo = keep.tile([P, H], F32, name="held_lo")
-        nc.scalar.copy(out=held_lo[:], in_=y_b[0][:, :H])
-        held_hi = keep.tile([P, CH], F32, name="held_hi")
-        nc.scalar.copy(out=held_hi[:], in_=y_b[1][:])
+        for q in TURNED:
+            yt[q] = keep.tile([P, BLOCKS, N], F32, name="yt%d" % q)
+            nc.scalar.copy(out=yt[q][:], in_=y[q][:])
 
-        def pick(nm, rows, c):
-            g = keep.tile([P, CH], F32, name="%s_picked%d" % (nm, c), tag="%s%d" % (nm, c))
-            nc.vector.tensor_copy(g[:], rows[:].indirect(offsets[:, c * CH // 16 : (c + 1) * CH // 16]))
+        def pick(nm, rows, q, on_vector):
+            g = keep.tile([P, Q], F32, name="%s%d" % (nm, q))
+            src = rows[:].indirect(offsets[:, q * Q // 16 : (q + 1) * Q // 16])
+            if on_vector:
+                nc.vector.tensor_copy(g[:], src)
+            else:
+                nc.scalar.activation(g[:], src, COPY)
             return g
 
-        identity = keep.tile([P, P], F32, name="identity")
-        make_identity(nc, identity[:])
-
-        def turn(nm, src, lo, blocks, bank):
-            dst = psum.tile([P, blocks * P], F32, name=nm, tag="bank%d" % bank)
-            for i in range(blocks):
-                nc.tensor.transpose(dst[:, i * P : (i + 1) * P], src[:, lo + i * P : lo + (i + 1) * P], identity[:])
+        def turn(nm, src, bank):
+            dst = psum.tile([P, BLOCKS, P], F32, name=nm, tag="bank%d" % bank)
+            for i in range(BLOCKS):
+                nc.tensor.transpose(dst[:, i, :], src[:, i * P : (i + 1) * P], identity[:])
             return dst
 
-        def turned_term(nm, h, q, angles, swap):
-            t = keep.tile([P, 2, P], F32, name="%s%d%d" % (nm, h, q), tag="%s%d%d" % (nm, h, q))
+        sums = {}
+
+        def turned_term(nm, h, q, angles, is_sin):
+            t = keep.tile([P, BLOCKS, P], F32, name="%s%d%d" % (nm, h, q))
+            src = h ^ is_sin
             nc.vector.scalar_tensor_tensor(
-                t[:],
-                yt[h ^ swap, q][:],
-                -1.0 if swap and h == 0 else 1.0,
-                angles[:].rearrange("p (i f) -> p i f", i=2),
-                MULT,
-                MULT,
+                t[:], yt[q][:, :, src * P : (src + 1) * P], -1.0 if is_sin and h == 0 else 1.0, angles[:], MULT, MULT
             )
-            for i in range(2):
+            for i in range(BLOCKS):
                 nc.tensor.matmul(
                     sums[h, q][:, i * P : (i + 1) * P],
                     t[:, i, :],
                     identity[:],
                     is_transpose=True,
-                    start=(not swap and i == 0),
-                    stop=(swap == 1 and i == 1),
+                    start=(not is_sin and i == 0),
+                    stop=(is_sin == 1 and i == BLOCKS - 1),
                 )
 
-        def product(eng, nm, factor, angles, tag):
-            t = keep.tile([P, H], F32, name=nm, tag=tag)
-            eng.tensor_tensor(t[:], factor, angles, MULT)
+        def product(nm, h, q, angles, is_sin):
+            t = keep.tile([P, Q], F32, name="%s%d%d" % (nm, h, q))
+            nc.vector.tensor_tensor(t[:], y[q][:, h ^ is_sin, :], angles[:], MULT)
             return t
 
-        turned_pieces = ((0, 0), (1, 0), (1, 1))
-        cos = [pick("cos", cos_rows, c) for c in range(CHUNKS)]
-        cos_turned = [turn("cos_turned%d" % q, cos[0], q * H, 2, 5 + q) for q in range(2)]
-        a_g0 = product(nc.gpsimd, "a_g0", held_a[:, 0, :], cos[0][:, H:], "a_g0")
-        a_g1 = product(nc.gpsimd, "a_g1", held_lo[:], cos[1][:, :H], "a_g1")
-        a_last = product(nc.gpsimd, "a_last", held_hi[:, H:], cos[1][:, H:], "a_last")
-        a_park = product(nc.vector, "a_park", y_b[0][:, H:], cos[1][:, H:], "a_park")
-        a_own = product(nc.vector, "a_own", y_b[1][:, :H], cos[1][:, :H], "a_own")
-        park_turned = turn("park_turned", a_park, 0, 2, 7)
-        staged = keep.tile([P, H], F32, name="staged")
-        nc.scalar.copy(out=staged[:], in_=park_turned[:])
-        sums = {}
-        for bank, (h, q) in enumerate(turned_pieces):
-            sums[h, q] = psum.tile([P, H], F32, name="sum%d%d" % (h, q), tag="bank%d" % (2 + bank))
-            turned_term("at", h, q, cos_turned[q], 0)
-        parked = turn("parked", staged, 0, 2, 7)
+        def store(h, q, r):
+            nc.sync.dma_start(out=out[h * P : (h + 1) * P, q * Q : (q + 1) * Q], in_=r[:])
 
-        def finish(eng, nm, h, cos_term, sin_term, lo, tag=None):
-            r = keep.tile([P, H], F32, name=nm, tag=tag or nm)
+        def finish(eng, h, q, cos_term, sin_term):
+            r = keep.tile([P, Q], F32, name="res%d%d" % (h, q))
             eng.tensor_tensor(r[:], cos_term, sin_term, SUB if h == 0 else ADD)
-            nc.sync.dma_start(out=out[h * P : (h + 1) * P, lo : lo + H], in_=r[:])
-
-        sin = [pick("sin", sin_rows, c) for c in range(CHUNKS)]
-        sin_turned = [turn("sin_turned%d" % q, sin[0], q * H, 2, 5 + q) for q in range(2)]
-        t_g0 = product(nc.gpsimd, "t_g0", held_a[:, 1, :], sin[0][:, H:], "t_g0")
-        finish(nc.gpsimd, "res_g0", 0, a_g0[:], t_g0[:], H)
-        t_g1 = product(nc.gpsimd, "t_g1", held_hi[:, :H], sin[1][:, :H], "sin0")
+            store(h, q, r)
 
         def finish_turned(h, q):
-            turned_term("tt", h, q, sin_turned[q], 1)
-            r = keep.tile([P, H], F32, name="res_turned%d%d" % (h, q))
+            r = keep.tile([P, Q], F32, name="res%d%d" % (h, q))
             nc.scalar.copy(out=r[:], in_=sums[h, q][:])
-            nc.sync.dma_start(out=out[h * P : (h + 1) * P, q * H : (q + 1) * H], in_=r[:])
+            store(h, q, r)
 
+        cos = {3: pick("cos", cos_rows, 3, True), 0: pick("cos", cos_rows, 0, False), 1: pick("cos", cos_rows, 1, False)}
+        cos[2] = pick("cos", cos_rows, 2, False)
+        a = {(h, 3): product("a", h, 3, cos[3], 0) for h in (1, 0)}
+        staged_bank = turn("staged_bank", a[1, 3], 7)
+        staged = keep.tile([P, Q], F32, name="staged")
+        nc.scalar.copy(out=staged[:], in_=staged_bank[:].rearrange("p i f -> p (i f)"))
+        sum_bank = {(0, 0): 0, (1, 0): 1, (0, 1): 4, (1, 1): 5}
+        for q in TURNED:
+            cos_turned = turn("cos_turned%d" % q, cos[q], 6)
+            for h in range(HALVES):
+                sums[h, q] = psum.tile([P, Q], F32, name="sum%d%d" % (h, q), tag="bank%d" % sum_bank[h, q])
+                turned_term("at", h, q, cos_turned, 0)
+        parked = turn("parked", staged, 7)
+        for h in range(HALVES):
+            a[h, 2] = product("a", h, 2, cos[2], 0)
+
+        sin = {2: pick("sin", sin_rows, 2, True)}
+        for q in (0, 1, 3):
+            sin[q] = pick("sin", sin_rows, q, False)
+        sin_turned0 = turn("sin_turned0", sin[0], 6)
+        t = {(h, 2): product("t", h, 2, sin[2], 1) for h in range(HALVES)}
+        finish(nc.gpsimd, 0, 2, a[0, 2][:], t[0, 2][:])
+        sin_turned1 = turn("sin_turned1", sin[1], 2)
+        turned_term("tt", 0, 0, sin_turned0, 1)
+        turned_term("tt", 1, 0, sin_turned0, 1)
         finish_turned(0, 0)
-        t_b = product(nc.vector, "t_b", y_b[1][:, H:], sin[1][:, H:], "yt10")
+        finish(nc.gpsimd, 1, 2, a[1, 2][:], t[1, 2][:])
         finish_turned(1, 0)
-        finish(nc.vector, "res_b", 0, parked[:], t_b[:], CH + H)
+        turned_term("tt", 0, 1, sin_turned1, 1)
+        turned_term("tt", 1, 1, sin_turned1, 1)
+        finish_turned(0, 1)
+        t[0, 3] = product("t", 0, 3, sin[3], 1)
+        t[1, 3] = product("t", 1, 3, sin[3], 1)
         finish_turned(1, 1)
-        t_a = product(nc.vector, "t_a", y_b[0][:, :H], sin[1][:, :H], "yt00")
-        t_c = product(nc.vector, "t_c", y_b[0][:, H:], sin[1][:, H:], "yt01")
-        finish(nc.vector, "res_g1", 0, a_g1[:], t_g1[:], CH, "tt10")
-        joint = keep.tile([P, CH], F32, name="joint")
-        nc.vector.tensor_tensor(joint[:, :H], a_own[:], t_a[:], ADD)
-        nc.vector.tensor_tensor(joint[:, H:], a_last[:], t_c[:], ADD)
-        nc.sync.dma_start(out=out[P:, CH:], in_=joint[:])
+        finish(nc.vector, 1, 3, parked[:].rearrange("p i f -> p (i f)"), t[1, 3][:])
+        finish(nc.gpsimd, 0, 3, a[0, 3][:], t[0, 3][:])

@@ -120,45 +120,55 @@ def tile_picked_zrope_none_p_kernel(tc, x_words, x_scales, w1, ct, st, offs, out
                 stop=stop,
             )
 
-        TURNED, PLAIN = (0, 1), (2, 3)
+        QT, QP, R1, R2 = 0, 1, 2, 3
         y = {q: psum.tile([P, 2, Q], F32, name="y%d" % q, tag="bank%d" % q) for q in range(4)}
         for o in range(PASSES):
             for q in range(4):
                 for i in range(2):
-                    first, last = (o == 0 and i == 0), (o == PASSES - 1 and i == 1)
-                    if q in TURNED:
+                    if q == QT:
                         lo = q * Q + i * P
-                        mx(y[q][:, i, :], o, slice(lo, lo + P), slice(o * N, (o + 1) * N), True, first, last)
+                        mx(y[q][:, i, :], o, slice(lo, lo + P), slice(o * N, (o + 1) * N), True, o + i == 0, o + i == 2)
                     else:
                         wc = slice(o * N + i * P, o * N + (i + 1) * P)
-                        mx(y[q][:, i, :], o, slice(q * Q, (q + 1) * Q), wc, False, first, last)
-        yt = {}
-        for q in TURNED:
-            yt[q] = keep.tile([P, BLOCKS, N], F32, name="yt%d" % q)
-            nc.scalar.copy(out=yt[q][:], in_=y[q][:])
+                        mx(y[q][:, i, :], o, slice(q * Q, (q + 1) * Q), wc, False, o + i == 0, o + i == 2)
+        yt3 = keep.tile([P, BLOCKS, 3, P], F32, name="yt3")
+        nc.scalar.copy(out=yt3[:, :, 1:, :].rearrange("p i h f -> p i (h f)"), in_=y[QT][:])
+        nc.scalar.activation(yt3[:, :, 0, :], y[QT][:, :, P:], COPY, scale=-1.0)
+        yt = {QT: yt3[:, :, 1:, :].rearrange("p i h f -> p i (h f)")}
+        held = [keep.tile([P, Q], F32, name="held%d" % h) for h in range(HALVES)]
+        for h in range(HALVES):
+            nc.scalar.copy(out=held[h][:], in_=y[QP][:, h, :])
 
-        def pick(nm, rows, q, on_vector):
-            g = keep.tile([P, Q], F32, name="%s%d" % (nm, q))
-            src = rows[:].indirect(offsets[:, q * Q // 16 : (q + 1) * Q // 16])
-            if on_vector:
-                nc.vector.tensor_copy(g[:], src)
-            else:
-                nc.scalar.activation(g[:], src, COPY)
+        def pick(nm, rows, q, on_vector, pieces=1):
+            g = keep.tile([P, Q], F32, name="%s%d" % (nm, q), tag="%s%d" % (nm, q))
+            w = Q // pieces
+            for i in range(pieces):
+                src = rows[:].indirect(offsets[:, (q * Q + i * w) // 16 : (q * Q + (i + 1) * w) // 16])
+                if on_vector:
+                    nc.vector.tensor_copy(g[:, i * w : (i + 1) * w], src)
+                else:
+                    nc.scalar.activation(g[:, i * w : (i + 1) * w], src, COPY)
             return g
 
-        def turn(nm, src, bank):
-            dst = psum.tile([P, BLOCKS, P], F32, name=nm, tag="bank%d" % bank)
+        def turn(dst, src):
             for i in range(BLOCKS):
-                nc.tensor.transpose(dst[:, i, :], src[:, i * P : (i + 1) * P], identity[:])
-            return dst
+                nc.tensor.transpose(dst[:, i * P : (i + 1) * P], src[:, i * P : (i + 1) * P], identity[:])
+
+        def bank(nm, b, width=Q):
+            return psum.tile([P, width], F32, name=nm, tag="bank%d" % b)
 
         sums = {}
 
         def turned_term(nm, h, q, angles, is_sin):
-            t = keep.tile([P, BLOCKS, P], F32, name="%s%d%d" % (nm, h, q))
+            t = keep.tile([P, BLOCKS, P], F32, name="%s%d%d" % (nm, h, q), tag="%s%d%d" % (nm, h, q))
             src = h ^ is_sin
             nc.vector.scalar_tensor_tensor(
-                t[:], yt[q][:, :, src * P : (src + 1) * P], -1.0 if is_sin and h == 0 else 1.0, angles[:], MULT, MULT
+                t[:],
+                yt[q][:, :, src * P : (src + 1) * P],
+                -1.0 if is_sin and h == 0 else 1.0,
+                angles[:].rearrange("p (i f) -> p i f", i=BLOCKS),
+                MULT,
+                MULT,
             )
             for i in range(BLOCKS):
                 nc.tensor.matmul(
@@ -170,57 +180,78 @@ def tile_picked_zrope_none_p_kernel(tc, x_words, x_scales, w1, ct, st, offs, out
                     stop=(is_sin == 1 and i == BLOCKS - 1),
                 )
 
-        def product(nm, h, q, angles, is_sin):
-            t = keep.tile([P, Q], F32, name="%s%d%d" % (nm, h, q))
-            nc.vector.tensor_tensor(t[:], y[q][:, h ^ is_sin, :], angles[:], MULT)
-            return t
+        def fresh(nm, tag=None):
+            return keep.tile([P, Q], F32, name=nm, tag=tag or nm)[:]
+
+        def product(dst, factor, angles):
+            nc.vector.tensor_tensor(dst, factor, angles[:], MULT)
+            return dst
 
         def store(h, q, r):
-            nc.sync.dma_start(out=out[h * P : (h + 1) * P, q * Q : (q + 1) * Q], in_=r[:])
+            nc.sync.dma_start(out=out[h * P : (h + 1) * P, q * Q : (q + 1) * Q], in_=r)
 
-        def finish(eng, h, q, cos_term, sin_term):
-            r = keep.tile([P, Q], F32, name="res%d%d" % (h, q))
-            eng.tensor_tensor(r[:], cos_term, sin_term, SUB if h == 0 else ADD)
-            store(h, q, r)
+        def finish(eng, dst, h, q, cos_term, sin_term):
+            eng.tensor_tensor(dst, cos_term, sin_term, SUB if h == 0 else ADD)
+            store(h, q, dst)
 
         def finish_turned(h, q):
-            r = keep.tile([P, Q], F32, name="res%d%d" % (h, q))
-            nc.scalar.copy(out=r[:], in_=sums[h, q][:])
+            r = fresh("res%d%d" % (h, q))
+            nc.scalar.copy(out=r, in_=sums[h, q][:])
             store(h, q, r)
 
-        cos = {3: pick("cos", cos_rows, 3, True), 0: pick("cos", cos_rows, 0, False), 1: pick("cos", cos_rows, 1, False)}
-        cos[2] = pick("cos", cos_rows, 2, False)
-        a = {(h, 3): product("a", h, 3, cos[3], 0) for h in (1, 0)}
-        staged_bank = turn("staged_bank", a[1, 3], 7)
+        cos = {q: pick("cos", cos_rows, q, q == R1) for q in (R1, QT, QP, R2)}
+        staged_bank = bank("staged_bank", 7)
+        turn(staged_bank, product(fresh("a_a0"), y[R1][:, 0, :], cos[R1]))
+        a = {(1, R1): product(fresh("a_a1"), y[R1][:, 1, :], cos[R1])}
         staged = keep.tile([P, Q], F32, name="staged")
-        nc.scalar.copy(out=staged[:], in_=staged_bank[:].rearrange("p i f -> p (i f)"))
-        sum_bank = {(0, 0): 0, (1, 0): 1, (0, 1): 4, (1, 1): 5}
-        for q in TURNED:
-            cos_turned = turn("cos_turned%d" % q, cos[q], 6)
-            for h in range(HALVES):
-                sums[h, q] = psum.tile([P, Q], F32, name="sum%d%d" % (h, q), tag="bank%d" % sum_bank[h, q])
-                turned_term("at", h, q, cos_turned, 0)
-        parked = turn("parked", staged, 7)
+        nc.scalar.copy(out=staged[:], in_=staged_bank[:])
+        cos_turned = bank("cos_turned", 6)
+        turn(cos_turned, cos[QT])
         for h in range(HALVES):
-            a[h, 2] = product("a", h, 2, cos[2], 0)
+            sums[h, QT] = bank("sum%d" % h, 4 + h)
+            turned_term("at", h, QT, cos_turned, 0)
+        for h in range(HALVES):
+            a[h, QP] = product(fresh("a_p%d" % h), held[h][:], cos[QP])
+        for h in range(HALVES):
+            a[h, R2] = product(fresh("a_b%d" % h), y[R2][:, h, :], cos[R2])
+        parked = bank("parked", 7)
+        turn(parked, staged)
 
-        sin = {2: pick("sin", sin_rows, 2, True)}
-        for q in (0, 1, 3):
+        t_p = [fresh("t_p%d" % h) for h in range(HALVES)]
+        for h in range(HALVES):
+            nc.vector.tensor_tensor(
+                t_p[h], sin_rows[:].indirect(offsets[:, QP * Q // 16 : (QP + 1) * Q // 16]), held[1 - h][:], MULT
+            )
+        sin = {QT: pick("sin", sin_rows, QT, False, 2)}
+        for q in (R1, R2):
             sin[q] = pick("sin", sin_rows, q, False)
-        sin_turned0 = turn("sin_turned0", sin[0], 6)
-        t = {(h, 2): product("t", h, 2, sin[2], 1) for h in range(HALVES)}
-        finish(nc.gpsimd, 0, 2, a[0, 2][:], t[0, 2][:])
-        sin_turned1 = turn("sin_turned1", sin[1], 2)
-        turned_term("tt", 0, 0, sin_turned0, 1)
-        turned_term("tt", 1, 0, sin_turned0, 1)
-        finish_turned(0, 0)
-        finish(nc.gpsimd, 1, 2, a[1, 2][:], t[1, 2][:])
-        finish_turned(1, 0)
-        turned_term("tt", 0, 1, sin_turned1, 1)
-        turned_term("tt", 1, 1, sin_turned1, 1)
-        finish_turned(0, 1)
-        t[0, 3] = product("t", 0, 3, sin[3], 1)
-        t[1, 3] = product("t", 1, 3, sin[3], 1)
-        finish_turned(1, 1)
-        finish(nc.vector, 1, 3, parked[:].rearrange("p i f -> p (i f)"), t[1, 3][:])
-        finish(nc.gpsimd, 0, 3, a[0, 3][:], t[0, 3][:])
+        sin_turned = [bank("sin_turned%d" % i, b, P) for i, b in enumerate((6, 1))]
+        for i in range(BLOCKS):
+            nc.tensor.transpose(sin_turned[i][:], sin[QT][:, i * P : (i + 1) * P], identity[:])
+        late = keep.tile([P, 4, Q], F32, name="late", tag="sin%d" % QT)
+        finish(nc.gpsimd, fresh("res_p0"), 0, QP, a[0, QP], t_p[0])
+        for i in range(BLOCKS):
+            t = keep.tile([P, HALVES, P], F32, name="tt%d" % i)
+            nc.vector.tensor_tensor(
+                t[:], yt3[:, i, :2, :], sin_turned[i][:].unsqueeze(1).to_broadcast([P, HALVES, P]), MULT
+            )
+            for h in range(HALVES):
+                nc.tensor.matmul(
+                    sums[h, QT][:, i * P : (i + 1) * P],
+                    t[:, h, :],
+                    identity[:],
+                    is_transpose=True,
+                    start=False,
+                    stop=(i == BLOCKS - 1),
+                )
+        t_a0 = product(late[:, 0, :], y[R1][:, 1, :], sin[R1])
+        t_a1 = product(late[:, 1, :], y[R1][:, 0, :], sin[R1])
+        finish(nc.vector, fresh("res_a0"), 0, R1, parked[:], t_a0)
+        finish(nc.gpsimd, fresh("res_p1"), 1, QP, a[1, QP], t_p[1])
+        finish_turned(0, QT)
+        t_b0 = product(late[:, 2, :], y[R2][:, 1, :], sin[R2])
+        finish_turned(1, QT)
+        t_b1 = product(late[:, 3, :], y[R2][:, 0, :], sin[R2])
+        finish(nc.vector, fresh("res_b0"), 0, R2, a[0, R2], t_b0)
+        finish(nc.gpsimd, fresh("res_a1"), 1, R1, a[1, R1], t_a1)
+        finish(nc.vector, fresh("res_b1"), 1, R2, a[1, R2], t_b1)

@@ -131,13 +131,20 @@ def tile_picked_zrope_none_p_kernel(tc, x_words, x_scales, w1, ct, st, offs, out
                     else:
                         wc = slice(o * N + i * P, o * N + (i + 1) * P)
                         mx(y[q][:, i, :], o, slice(q * Q, (q + 1) * Q), wc, False, o + i == 0, o + i == 2)
+        yt_bank = psum.tile([P, BLOCKS, N], F32, name="yt_bank", tag="bank4")
+        for o in range(PASSES):
+            for i in range(BLOCKS):
+                lo = R2 * Q + i * P
+                mx(yt_bank[:, i, :], o, slice(lo, lo + P), slice(o * N, (o + 1) * N), True, o + i == 0, o + i == 2)
         yt3 = keep.tile([P, BLOCKS, 3, P], F32, name="yt3")
         nc.scalar.copy(out=yt3[:, :, 1:, :].rearrange("p i h f -> p i (h f)"), in_=y[QT][:])
         nc.scalar.activation(yt3[:, :, 0, :], y[QT][:, :, P:], COPY, scale=-1.0)
         yt = {QT: yt3[:, :, 1:, :].rearrange("p i h f -> p i (h f)")}
+        yt[R2] = keep.tile([P, BLOCKS, N], F32, name="yt_b")
+        nc.vector.tensor_copy(yt[R2][:], yt_bank[:])
         held = [keep.tile([P, Q], F32, name="held%d" % h) for h in range(HALVES)]
         for h in range(HALVES):
-            nc.scalar.copy(out=held[h][:], in_=y[QP][:, h, :])
+            nc.vector.tensor_copy(held[h][:], y[QP][:, h, :])
 
         def pick(nm, rows, q, on_vector, pieces=1):
             g = keep.tile([P, Q], F32, name="%s%d" % (nm, q), tag="%s%d" % (nm, q))
@@ -199,21 +206,28 @@ def tile_picked_zrope_none_p_kernel(tc, x_words, x_scales, w1, ct, st, offs, out
             nc.scalar.copy(out=r, in_=sums[h, q][:])
             store(h, q, r)
 
-        cos = {q: pick("cos", cos_rows, q, q == R1) for q in (R1, QT, QP, R2)}
+        cos = {q: pick("cos", cos_rows, q, q == R1) for q in (R1, QT, R2, QP)}
         staged_bank = bank("staged_bank", 7)
         turn(staged_bank, product(fresh("a_a0"), y[R1][:, 0, :], cos[R1]))
         a = {(1, R1): product(fresh("a_a1"), y[R1][:, 1, :], cos[R1])}
         staged = keep.tile([P, Q], F32, name="staged")
         nc.scalar.copy(out=staged[:], in_=staged_bank[:])
-        cos_turned = bank("cos_turned", 6)
-        turn(cos_turned, cos[QT])
+        cos_turned = {QT: bank("cos_turned0", 6), R2: bank("cos_turned1", 1)}
+        for q in cos_turned:
+            turn(cos_turned[q], cos[q])
         for h in range(HALVES):
             sums[h, QT] = bank("sum%d" % h, 4 + h)
-            turned_term("at", h, QT, cos_turned, 0)
+            turned_term("at", h, QT, cos_turned[QT], 0)
+        parked_b = bank("parked_b", 0, 2 * Q)
+        for h in range(HALVES):
+            t = keep.tile([P, BLOCKS, P], F32, name="at_b%d" % h)
+            nc.vector.tensor_tensor(
+                t[:], yt[R2][:, :, h * P : (h + 1) * P], cos_turned[R2][:].rearrange("p (i f) -> p i f", i=BLOCKS), MULT
+            )
+            turn(parked_b[:, h * Q : (h + 1) * Q], t[:].rearrange("p i f -> p (i f)"))
+            a[h, R2] = parked_b[:, h * Q : (h + 1) * Q]
         for h in range(HALVES):
             a[h, QP] = product(fresh("a_p%d" % h), held[h][:], cos[QP])
-        for h in range(HALVES):
-            a[h, R2] = product(fresh("a_b%d" % h), y[R2][:, h, :], cos[R2])
         parked = bank("parked", 7)
         turn(parked, staged)
 

@@ -206,10 +206,10 @@ def tile_picked_zrope_none_p_kernel(tc, x_words, x_scales, w1, ct, st, offs, out
             nc.scalar.copy(out=r, in_=sums[h, q][:])
             store(h, q, r)
 
-        cos = {q: pick("cos", cos_rows, q, q == R1) for q in (R1, QT, R2, QP)}
+        cos = {q: pick("cos", cos_rows, q, q == QP) for q in (QP, QT, R2, R1)}
         staged_bank = bank("staged_bank", 7)
-        turn(staged_bank, product(fresh("a_a0"), y[R1][:, 0, :], cos[R1]))
-        a = {(1, R1): product(fresh("a_a1"), y[R1][:, 1, :], cos[R1])}
+        turn(staged_bank, product(fresh("a_p1"), held[1][:], cos[QP]))
+        a = {(0, QP): product(fresh("a_p0"), held[0][:], cos[QP])}
         staged = keep.tile([P, Q], F32, name="staged")
         nc.scalar.copy(out=staged[:], in_=staged_bank[:])
         cos_turned = {QT: bank("cos_turned0", 6), R2: bank("cos_turned1", 1)}
@@ -227,7 +227,7 @@ def tile_picked_zrope_none_p_kernel(tc, x_words, x_scales, w1, ct, st, offs, out
             turn(parked_b[:, h * Q : (h + 1) * Q], t[:].rearrange("p i f -> p (i f)"))
             a[h, R2] = parked_b[:, h * Q : (h + 1) * Q]
         for h in range(HALVES):
-            a[h, QP] = product(fresh("a_p%d" % h), held[h][:], cos[QP])
+            a[h, R1] = product(fresh("a_a%d" % h), y[R1][:, h, :], cos[R1])
         parked = bank("parked", 7)
         turn(parked, staged)
 
@@ -242,7 +242,7 @@ def tile_picked_zrope_none_p_kernel(tc, x_words, x_scales, w1, ct, st, offs, out
         sin_turned = [bank("sin_turned%d" % i, b, P) for i, b in enumerate((6, 1))]
         for i in range(BLOCKS):
             nc.tensor.transpose(sin_turned[i][:], sin[QT][:, i * P : (i + 1) * P], identity[:])
-        late = keep.tile([P, 4, Q], F32, name="late", tag="sin%d" % QT)
+        late = keep.tile([P, 5, Q], F32, name="late", tag="sin%d" % QT)
         finish(nc.gpsimd, fresh("res_p0"), 0, QP, a[0, QP], t_p[0])
         for i in range(BLOCKS):
             t = keep.tile([P, HALVES, P], F32, name="tt%d" % i)
@@ -259,13 +259,15 @@ def tile_picked_zrope_none_p_kernel(tc, x_words, x_scales, w1, ct, st, offs, out
                     stop=(i == BLOCKS - 1),
                 )
         t_a0 = product(late[:, 0, :], y[R1][:, 1, :], sin[R1])
-        t_a1 = product(late[:, 1, :], y[R1][:, 0, :], sin[R1])
-        finish(nc.vector, fresh("res_a0"), 0, R1, parked[:], t_a0)
-        finish(nc.gpsimd, fresh("res_p1"), 1, QP, a[1, QP], t_p[1])
+        finish(nc.vector, late[:, 4, :], 1, QP, parked[:], t_p[1])
+        finish(nc.vector, fresh("res_a0"), 0, R1, a[0, R1], t_a0)
         finish_turned(0, QT)
-        t_b0 = product(late[:, 2, :], y[R2][:, 1, :], sin[R2])
+        t_a1 = product(late[:, 1, :], y[R1][:, 0, :], sin[R1])
         finish_turned(1, QT)
+        t_b0 = product(late[:, 2, :], y[R2][:, 1, :], sin[R2])
+        joint = keep.tile([P, 2 * Q], F32, name="joint")
+        nc.gpsimd.tensor_tensor(joint[:, :Q], a[1, R1], t_a1, ADD)
         t_b1 = product(late[:, 3, :], y[R2][:, 0, :], sin[R2])
         finish(nc.vector, fresh("res_b0"), 0, R2, a[0, R2], t_b0)
-        finish(nc.gpsimd, fresh("res_a1"), 1, R1, a[1, R1], t_a1)
-        finish(nc.vector, fresh("res_b1"), 1, R2, a[1, R2], t_b1)
+        nc.vector.tensor_tensor(joint[:, Q:], a[1, R2], t_b1, ADD)
+        nc.sync.dma_start(out=out[P:, R1 * Q :], in_=joint[:])

@@ -136,10 +136,8 @@ def tile_picked_zrope_none_p_kernel(tc, x_words, x_scales, w1, ct, st, offs, out
             for i in range(BLOCKS):
                 lo = R2 * Q + i * P
                 mx(yt_bank[:, i, :], o, slice(lo, lo + P), slice(o * N, (o + 1) * N), True, o + i == 0, o + i == 2)
-        yt3 = keep.tile([P, BLOCKS, 3, P], F32, name="yt3")
-        nc.scalar.copy(out=yt3[:, :, 1:, :].rearrange("p i h f -> p i (h f)"), in_=y[QT][:])
-        nc.scalar.activation(yt3[:, :, 0, :], y[QT][:, :, P:], COPY, scale=-1.0)
-        yt = {QT: yt3[:, :, 1:, :].rearrange("p i h f -> p i (h f)")}
+        yt = {QT: keep.tile([P, BLOCKS, N], F32, name="yt", tag="yt")}
+        nc.scalar.copy(out=yt[QT][:], in_=y[QT][:])
         yt[R2] = keep.tile([P, BLOCKS, N], F32, name="yt_b")
         nc.vector.tensor_copy(yt[R2][:], yt_bank[:])
         held = [keep.tile([P, Q], F32, name="held%d" % h) for h in range(HALVES)]
@@ -194,17 +192,17 @@ def tile_picked_zrope_none_p_kernel(tc, x_words, x_scales, w1, ct, st, offs, out
             nc.vector.tensor_tensor(dst, factor, angles[:], MULT)
             return dst
 
-        def store(h, q, r):
-            nc.sync.dma_start(out=out[h * P : (h + 1) * P, q * Q : (q + 1) * Q], in_=r)
+        def store(h, q, r, queue=nc.sync):
+            queue.dma_start(out=out[h * P : (h + 1) * P, q * Q : (q + 1) * Q], in_=r)
 
-        def finish(eng, dst, h, q, cos_term, sin_term):
+        def finish(eng, dst, h, q, cos_term, sin_term, queue=nc.sync):
             eng.tensor_tensor(dst, cos_term, sin_term, SUB if h == 0 else ADD)
-            store(h, q, dst)
+            store(h, q, dst, queue)
 
-        def finish_turned(h, q):
-            r = fresh("res%d%d" % (h, q))
+        def finish_turned(h, q, tag=None, queue=nc.sync):
+            r = fresh("res%d%d" % (h, q), tag)
             nc.scalar.copy(out=r, in_=sums[h, q][:])
-            store(h, q, r)
+            store(h, q, r, queue)
 
         cos = {q: pick("cos", cos_rows, q, q == QP) for q in (QP, QT, R2, R1)}
         staged_bank = bank("staged_bank", 7)
@@ -244,30 +242,30 @@ def tile_picked_zrope_none_p_kernel(tc, x_words, x_scales, w1, ct, st, offs, out
             nc.tensor.transpose(sin_turned[i][:], sin[QT][:, i * P : (i + 1) * P], identity[:])
         late = keep.tile([P, 5, Q], F32, name="late", tag="sin%d" % QT)
         finish(nc.gpsimd, fresh("res_p0"), 0, QP, a[0, QP], t_p[0])
-        for i in range(BLOCKS):
-            t = keep.tile([P, HALVES, P], F32, name="tt%d" % i)
-            nc.vector.tensor_tensor(
-                t[:], yt3[:, i, :2, :], sin_turned[i][:].unsqueeze(1).to_broadcast([P, HALVES, P]), MULT
+
+        def block_term(h, i):
+            t = keep.tile([P, P], F32, name="tt%d%d" % (h, i))
+            nc.vector.scalar_tensor_tensor(
+                t[:], yt[QT][:, i, (1 - h) * P : (2 - h) * P], -1.0 if h == 0 else 1.0, sin_turned[i][:], MULT, MULT
             )
-            for h in range(HALVES):
-                nc.tensor.matmul(
-                    sums[h, QT][:, i * P : (i + 1) * P],
-                    t[:, h, :],
-                    identity[:],
-                    is_transpose=True,
-                    start=False,
-                    stop=(i == BLOCKS - 1),
-                )
+            nc.tensor.matmul(
+                sums[h, QT][:, i * P : (i + 1) * P], t[:], identity[:], is_transpose=True, start=False, stop=(i == BLOCKS - 1)
+            )
+
+        block_term(0, 0)
+        block_term(1, 0)
+        block_term(0, 1)
         t_a0 = product(late[:, 0, :], y[R1][:, 1, :], sin[R1])
+        block_term(1, 1)
         finish(nc.vector, late[:, 4, :], 1, QP, parked[:], t_p[1])
-        finish(nc.vector, fresh("res_a0"), 0, R1, a[0, R1], t_a0)
-        finish_turned(0, QT)
+        mid = keep.tile([P, 2, Q], F32, name="mid", tag="yt")
+        nc.scalar.copy(out=mid[:, 0, :], in_=sums[0, QT][:])
+        store(0, QT, mid[:, 0, :])
+        finish(nc.gpsimd, mid[:, 1, :], 0, R1, a[0, R1], t_a0)
         t_a1 = product(late[:, 1, :], y[R1][:, 0, :], sin[R1])
         finish_turned(1, QT)
         t_b0 = product(late[:, 2, :], y[R2][:, 1, :], sin[R2])
-        joint = keep.tile([P, 2 * Q], F32, name="joint")
-        nc.gpsimd.tensor_tensor(joint[:, :Q], a[1, R1], t_a1, ADD)
         t_b1 = product(late[:, 3, :], y[R2][:, 0, :], sin[R2])
         finish(nc.vector, fresh("res_b0"), 0, R2, a[0, R2], t_b0)
-        nc.vector.tensor_tensor(joint[:, Q:], a[1, R2], t_b1, ADD)
-        nc.sync.dma_start(out=out[P:, R1 * Q :], in_=joint[:])
+        finish(nc.gpsimd, fresh("res_a1"), 1, R1, a[1, R1], t_a1, nc.scalar)
+        finish(nc.vector, fresh("res_b1"), 1, R2, a[1, R2], t_b1)

@@ -33,18 +33,8 @@ def tile_picked_zrope_none_p_kernel(tc, x_words, x_scales, w1, ct, st, offs, out
         psum = ctx.enter_context(tc.psum_pool(name="psum", bufs=1))
 
         scale_rows = keep.tile([P, T], U8, name="scale_rows", tag="early_a", align_bytes=64)
-        x_planes = [keep.tile([P, S], U8, name="x_plane%d" % o, align_bytes=64) for o in range(PASSES)]
         nc.vector.memset(scale_rows[:, : T // 2].bitcast(I32), 0)
         nc.gpsimd.memset(scale_rows[:, T // 2 :].bitcast(I32), 0)
-        for plane in x_planes:
-            nc.vector.memset(plane[:].bitcast(I32), 0)
-
-        w_rows = w1.rearrange("(o p j) n -> o p (j n)", o=PASSES, j=PACK)
-
-        def load_w(o):
-            t = keep.tile([P, PACK, N], F32, name="w_raw%d" % o)
-            nc.sync.dma_start(out=t[:].rearrange("p j n -> p (j n)"), in_=w_rows[o])
-            return t
 
         def load_words(o, tag):
             t = keep.tile([P, T], U32, name="words%d" % o, tag=tag, align_bytes=64)
@@ -54,18 +44,26 @@ def tile_picked_zrope_none_p_kernel(tc, x_words, x_scales, w1, ct, st, offs, out
             )
             return t
 
-        w_raw = [load_w(0)]
+        w_rows = w1.rearrange("(o p j) n -> o p (j n)", o=PASSES, j=PACK)
+        w_raw = [keep.tile([P, PACK, N], F32, name="w_raw%d" % o) for o in range(PASSES)]
+        nc.sync.dma_start(out=w_raw[0][:].rearrange("p j n -> p (j n)"), in_=w_rows[0])
         offsets = keep.tile([P, S // 16], U16, name="offsets")
         nc.sync.dma_start(offsets[:], offs)
-        nc.sync.dma_start(
-            out=scale_rows[0:P:4, :].bitcast(I32),
-            in_=x_scales.rearrange("o q c -> (o q) c").bitcast(I32),
-        )
-        w_raw.append(load_w(1))
-        words = [load_words(0, "early_c")]
+        for o in range(PASSES):
+            nc.sync.dma_start(out=scale_rows[4 * o : P : 8, :].bitcast(I32), in_=x_scales[o].bitcast(I32))
+        nc.sync.dma_start(out=w_raw[1][:].rearrange("p j n -> p (j n)"), in_=w_rows[1])
+        words = [load_words(0, "early_c"), load_words(1, "words1")]
 
         picked_rows = keep.tile([P, S], U8, name="picked_rows", align_bytes=64)
         nc.vector.tensor_copy(picked_rows[:], scale_rows[:].indirect(offsets[:]))
+        x_planes = keep.tile([P, S], U8, name="x_planes", align_bytes=64)
+        nc.vector.tensor_copy(x_planes[:].bitcast(I32), picked_rows[:].bitcast(I32))
+        for o in range(PASSES):
+            for j in range(1, 4):
+                nc.sync.dma_start(
+                    out=x_planes[4 * o + j : P : 32, :].bitcast(I32),
+                    in_=picked_rows[8 * j + 4 * o : P : 32, :].bitcast(I32),
+                )
 
         w_grouped = keep.tile([P, PASSES, N, PACK], BF16, name="w_grouped", tag="early_b", align_bytes=64)
         for o in range(PASSES):
@@ -77,19 +75,6 @@ def tile_picked_zrope_none_p_kernel(tc, x_words, x_scales, w1, ct, st, offs, out
             scales=w_planes[:],
             in_=w_grouped[:].rearrange("p o n j -> p (o n j)"),
         )
-
-        def move(o, j):
-            nc.sync.dma_start(
-                out=x_planes[o][4 * o + j : P : 32, :].bitcast(I32),
-                in_=picked_rows[64 * o + 4 * j : 64 * (o + 1) : 16, :].bitcast(I32),
-            )
-
-        moves = [(o, j) for o in range(PASSES) for j in range(4)]
-        for o, j in moves[:2]:
-            move(o, j)
-        words.append(load_words(1, "early_a"))
-        for o, j in moves[2:]:
-            move(o, j)
         cos_rows = keep.tile([P, T], F32, name="cos_rows", tag="early_b", align_bytes=64)
         nc.sync.dma_start(out=cos_rows[:], in_=ct[0:P, :])
 
@@ -107,7 +92,7 @@ def tile_picked_zrope_none_p_kernel(tc, x_words, x_scales, w1, ct, st, offs, out
         make_identity(nc, identity[:])
 
         def mx(dst, o, cols, wc, tokens_stationary, start, stop):
-            x_side = (picked[o][:, cols].bitcast(FP8X4), x_planes[o][4 * o :, cols])
+            x_side = (picked[o][:, cols].bitcast(FP8X4), x_planes[4 * o :, cols])
             w_side = (w_codes[:, wc].bitcast(FP8X4), w_planes[:, wc])
             still, moving = (x_side, w_side) if tokens_stationary else (w_side, x_side)
             nc.tensor.matmul_mx(
@@ -120,7 +105,7 @@ def tile_picked_zrope_none_p_kernel(tc, x_words, x_scales, w1, ct, st, offs, out
                 stop=stop,
             )
 
-        QT, QP, R1, R2 = 0, 1, 2, 3
+        QP, QT, R1, R2 = 0, 1, 2, 3
         y = {q: psum.tile([P, 2, Q], F32, name="y%d" % q, tag="bank%d" % q) for q in range(4)}
         for o in range(PASSES):
             for q in range(4):
@@ -255,17 +240,19 @@ def tile_picked_zrope_none_p_kernel(tc, x_words, x_scales, w1, ct, st, offs, out
         block_term(0, 0)
         block_term(1, 0)
         block_term(0, 1)
-        t_a0 = product(late[:, 0, :], y[R1][:, 1, :], sin[R1])
+        t_a1 = product(late[:, 0, :], y[R1][:, 0, :], sin[R1])
         block_term(1, 1)
         finish(nc.vector, late[:, 4, :], 1, QP, parked[:], t_p[1])
-        mid = keep.tile([P, 2, Q], F32, name="mid", tag="yt")
-        nc.scalar.copy(out=mid[:, 0, :], in_=sums[0, QT][:])
-        store(0, QT, mid[:, 0, :])
-        finish(nc.gpsimd, mid[:, 1, :], 0, R1, a[0, R1], t_a0)
-        t_a1 = product(late[:, 1, :], y[R1][:, 0, :], sin[R1])
-        finish_turned(1, QT)
-        t_b0 = product(late[:, 2, :], y[R2][:, 1, :], sin[R2])
-        t_b1 = product(late[:, 3, :], y[R2][:, 0, :], sin[R2])
-        finish(nc.vector, fresh("res_b0"), 0, R2, a[0, R2], t_b0)
-        finish(nc.gpsimd, fresh("res_a1"), 1, R1, a[1, R1], t_a1, nc.scalar)
+        finish_turned(0, QT, "yt")
+        joint_hi = keep.tile([P, 2 * Q], F32, name="joint_hi")
+        nc.scalar.copy(out=joint_hi[:, :Q], in_=sums[1, QT][:])
+        nc.gpsimd.tensor_tensor(joint_hi[:, Q:], a[1, R1], t_a1, ADD)
+        nc.sync.dma_start(out=out[P:, QT * Q : (R1 + 1) * Q], in_=joint_hi[:])
+        t_a0 = product(late[:, 1, :], y[R1][:, 1, :], sin[R1])
+        joint_lo = keep.tile([P, 2 * Q], F32, name="joint_lo")
+        nc.gpsimd.tensor_tensor(joint_lo[:, :Q], a[0, R1], t_a0, SUB)
+        t_b1 = product(late[:, 2, :], y[R2][:, 0, :], sin[R2])
+        t_b0 = product(late[:, 3, :], y[R2][:, 1, :], sin[R2])
         finish(nc.vector, fresh("res_b1"), 1, R2, a[1, R2], t_b1)
+        nc.vector.tensor_tensor(joint_lo[:, Q:], a[0, R2], t_b0, SUB)
+        nc.sync.dma_start(out=out[:P, R1 * Q :], in_=joint_lo[:])

from contextlib import ExitStack

import concourse.mybir as mybir
from concourse.masks import make_identity

K, T, S, N = 1024, 4096, 1024, 256
FLOPS = 2 * K * S * N
BYTES = K * T + K * T // 32 + 4 * K * N + 2 * 4 * (N // 2) * T + 2 * 128 * S // 16 + 4 * N * S
P = 128
PACK = 4
PASSES = K // (P * PACK)
HALVES = N // P
Q = 256
BLOCKS = Q // P

F32 = mybir.dt.float32
BF16 = mybir.dt.bfloat16
I32 = mybir.dt.int32
U32 = mybir.dt.uint32
U16 = mybir.dt.uint16
U8 = mybir.dt.uint8
FP8X4 = mybir.dt.float8_e4m3fn_x4
MULT = mybir.AluOpType.mult
ADD = mybir.AluOpType.add
SUB = mybir.AluOpType.subtract
COPY = mybir.ActivationFunctionType.Copy


def tile_picked_zrope_none_p_kernel(tc, x_words, x_scales, w1, ct, st, offs, out):
    nc = tc.nc
    with ExitStack() as ctx:
        keep = ctx.enter_context(tc.tile_pool(name="keep", bufs=1))
        psum = ctx.enter_context(tc.psum_pool(name="psum", bufs=1))

        scale_rows = keep.tile([P, T], U8, name="scale_rows", tag="early_a", align_bytes=64)
        nc.vector.memset(scale_rows[:, : T // 2].bitcast(I32), 0)
        nc.gpsimd.memset(scale_rows[:, T // 2 :].bitcast(I32), 0)

        def load_words(o, tag):
            t = keep.tile([P, T], U32, name="words%d" % o, tag=tag, align_bytes=64)
            nc.sync.dma_start(
                out=t[:].bitcast(I32),
                in_=x_words[o].rearrange("p c r -> p (c r)").bitcast(I32),
            )
            return t

        w_rows = w1.rearrange("(o p j) n -> o p (j n)", o=PASSES, j=PACK)
        w_raw = [keep.tile([P, PACK, N], F32, name="w_raw%d" % o) for o in range(PASSES)]
        nc.sync.dma_start(out=w_raw[0][:].rearrange("p j n -> p (j n)"), in_=w_rows[0])
        offsets = keep.tile([P, S // 16], U16, name="offsets")
        nc.sync.dma_start(offsets[:], offs)
        for o in range(PASSES):
            nc.sync.dma_start(out=scale_rows[4 * o : P : 8, :].bitcast(I32), in_=x_scales[o].bitcast(I32))
        nc.sync.dma_start(out=w_raw[1][:].rearrange("p j n -> p (j n)"), in_=w_rows[1])
        words = [load_words(0, "early_c"), load_words(1, "words1")]

        picked_rows = keep.tile([P, S], U8, name="picked_rows", align_bytes=64)
        nc.vector.tensor_copy(picked_rows[:], scale_rows[:].indirect(offsets[:]))
        x_planes = keep.tile([P, S], U8, name="x_planes", align_bytes=64)
        nc.vector.tensor_copy(x_planes[:].bitcast(I32), picked_rows[:].bitcast(I32))
        for o in range(PASSES):
            for j in range(1, 4):
                nc.sync.dma_start(
                    out=x_planes[4 * o + j : P : 32, :].bitcast(I32),
                    in_=picked_rows[8 * j + 4 * o : P : 32, :].bitcast(I32),
                )

        w_grouped = keep.tile([P, PASSES, N, PACK], BF16, name="w_grouped", tag="early_b", align_bytes=64)
        for o in range(PASSES):
            nc.scalar.copy(out=w_grouped[:, o], in_=w_raw[o][:].rearrange("p j n -> p n j"))
        w_codes = keep.tile([P, PASSES * N], U32, name="w_codes", align_bytes=64)
        w_planes = keep.tile([P, PASSES * N], U8, name="w_planes", align_bytes=64)
        nc.vector.quantize_mx(
            out=w_codes[:].bitcast(FP8X4),
            scales=w_planes[:],
            in_=w_grouped[:].rearrange("p o n j -> p (o n j)"),
        )
        cos_rows = keep.tile([P, T], F32, name="cos_rows", tag="early_b", align_bytes=64)
        nc.sync.dma_start(out=cos_rows[:], in_=ct[0:P, :])

        picked = [keep.tile([P, S], U32, name="picked%d" % o, align_bytes=64) for o in range(PASSES)]
        nc.vector.tensor_copy(picked[0][:], words[0][:].indirect(offsets[:]))
        for c in range(2):
            nc.vector.tensor_copy(
                picked[1][:, c * S // 2 : (c + 1) * S // 2],
                words[1][:].indirect(offsets[:, c * S // 32 : (c + 1) * S // 32]),
            )
        sin_rows = keep.tile([P, T], F32, name="sin_rows", tag="early_c", align_bytes=64)
        nc.sync.dma_start(out=sin_rows[:], in_=st[0:P, :])

        identity = keep.tile([P, P], F32, name="identity")
        make_identity(nc, identity[:])

        def mx(dst, o, cols, wc, tokens_stationary, start, stop):
            x_side = (picked[o][:, cols].bitcast(FP8X4), x_planes[4 * o :, cols])
            w_side = (w_codes[:, wc].bitcast(FP8X4), w_planes[:, wc])
            still, moving = (x_side, w_side) if tokens_stationary else (w_side, x_side)
            nc.tensor.matmul_mx(
                out=dst,
                lhsT=still[0],
                lhsT_scale=still[1],
                rhs=moving[0],
                rhs_scale=moving[1],
                start=start,
                stop=stop,
            )

        QP, QT, R1, R2 = 0, 1, 2, 3
        y = {q: psum.tile([P, 2, Q], F32, name="y%d" % q, tag="bank%d" % q) for q in range(4)}
        for o in range(PASSES):
            for q in range(4):
                for i in range(2):
                    if q == QT:
                        lo = q * Q + i * P
                        mx(y[q][:, i, :], o, slice(lo, lo + P), slice(o * N, (o + 1) * N), True, o + i == 0, o + i == 2)
                    else:
                        wc = slice(o * N + i * P, o * N + (i + 1) * P)
                        mx(y[q][:, i, :], o, slice(q * Q, (q + 1) * Q), wc, False, o + i == 0, o + i == 2)
        yt_bank = psum.tile([P, BLOCKS, N], F32, name="yt_bank", tag="bank4")
        for o in range(PASSES):
            for i in range(BLOCKS):
                lo = R2 * Q + i * P
                mx(yt_bank[:, i, :], o, slice(lo, lo + P), slice(o * N, (o + 1) * N), True, o + i == 0, o + i == 2)
        yt = {QT: keep.tile([P, BLOCKS, N], F32, name="yt", tag="yt")}
        nc.scalar.copy(out=yt[QT][:], in_=y[QT][:])
        yt[R2] = keep.tile([P, BLOCKS, N], F32, name="yt_b")
        nc.vector.tensor_copy(yt[R2][:], yt_bank[:])
        held = [keep.tile([P, Q], F32, name="held%d" % h) for h in range(HALVES)]
        for h in range(HALVES):
            nc.vector.tensor_copy(held[h][:], y[QP][:, h, :])

        def pick(nm, rows, q, on_vector, pieces=1):
            g = keep.tile([P, Q], F32, name="%s%d" % (nm, q), tag="%s%d" % (nm, q))
            w = Q // pieces
            for i in range(pieces):
                src = rows[:].indirect(offsets[:, (q * Q + i * w) // 16 : (q * Q + (i + 1) * w) // 16])
                if on_vector:
                    nc.vector.tensor_copy(g[:, i * w : (i + 1) * w], src)
                else:
                    nc.scalar.activation(g[:, i * w : (i + 1) * w], src, COPY)
            return g

        def turn(dst, src):
            for i in range(BLOCKS):
                nc.tensor.transpose(dst[:, i * P : (i + 1) * P], src[:, i * P : (i + 1) * P], identity[:])

        def bank(nm, b, width=Q):
            return psum.tile([P, width], F32, name=nm, tag="bank%d" % b)

        sums = {}

        def turned_term(nm, h, q, angles, is_sin):
            t = keep.tile([P, BLOCKS, P], F32, name="%s%d%d" % (nm, h, q), tag="%s%d%d" % (nm, h, q))
            src = h ^ is_sin
            nc.vector.scalar_tensor_tensor(
                t[:],
                yt[q][:, :, src * P : (src + 1) * P],
                -1.0 if is_sin and h == 0 else 1.0,
                angles[:].rearrange("p (i f) -> p i f", i=BLOCKS),
                MULT,
                MULT,
            )
            for i in range(BLOCKS):
                nc.tensor.matmul(
                    sums[h, q][:, i * P : (i + 1) * P],
                    t[:, i, :],
                    identity[:],
                    is_transpose=True,
                    start=(not is_sin and i == 0),
                    stop=(is_sin == 1 and i == BLOCKS - 1),
                )

        def fresh(nm, tag=None):
            return keep.tile([P, Q], F32, name=nm, tag=tag or nm)[:]

        def product(dst, factor, angles):
            nc.vector.tensor_tensor(dst, factor, angles[:], MULT)
            return dst

        def store(h, q, r, queue=nc.sync):
            queue.dma_start(out=out[h * P : (h + 1) * P, q * Q : (q + 1) * Q], in_=r)

        def finish(eng, dst, h, q, cos_term, sin_term, queue=nc.sync):
            eng.tensor_tensor(dst, cos_term, sin_term, SUB if h == 0 else ADD)
            store(h, q, dst, queue)

        def finish_turned(h, q, tag=None, queue=nc.sync):
            r = fresh("res%d%d" % (h, q), tag)
            nc.scalar.copy(out=r, in_=sums[h, q][:])
            store(h, q, r, queue)

        cos = {q: pick("cos", cos_rows, q, q == QP) for q in (QP, QT, R2, R1)}
        staged_bank = bank("staged_bank", 7)
        turn(staged_bank, product(fresh("a_p1"), held[1][:], cos[QP]))
        a = {(0, QP): product(fresh("a_p0"), held[0][:], cos[QP])}
        staged = keep.tile([P, Q], F32, name="staged")
        nc.scalar.copy(out=staged[:], in_=staged_bank[:])
        cos_turned = {QT: bank("cos_turned0", 6), R2: bank("cos_turned1", 1)}
        for q in cos_turned:
            turn(cos_turned[q], cos[q])
        for h in range(HALVES):
            sums[h, QT] = bank("sum%d" % h, 4 + h)
            turned_term("at", h, QT, cos_turned[QT], 0)
        parked_b = bank("parked_b", 0, 2 * Q)
        for h in range(HALVES):
            t = keep.tile([P, BLOCKS, P], F32, name="at_b%d" % h)
            nc.vector.tensor_tensor(
                t[:], yt[R2][:, :, h * P : (h + 1) * P], cos_turned[R2][:].rearrange("p (i f) -> p i f", i=BLOCKS), MULT
            )
            turn(parked_b[:, h * Q : (h + 1) * Q], t[:].rearrange("p i f -> p (i f)"))
            a[h, R2] = parked_b[:, h * Q : (h + 1) * Q]
        for h in range(HALVES):
            a[h, R1] = product(fresh("a_a%d" % h), y[R1][:, h, :], cos[R1])
        parked = bank("parked", 7)
        turn(parked, staged)

        t_p = [fresh("t_p%d" % h) for h in range(HALVES)]
        for h in range(HALVES):
            nc.vector.tensor_tensor(
                t_p[h], sin_rows[:].indirect(offsets[:, QP * Q // 16 : (QP + 1) * Q // 16]), held[1 - h][:], MULT
            )
        sin = {QT: pick("sin", sin_rows, QT, False, 2)}
        for q in (R1, R2):
            sin[q] = pick("sin", sin_rows, q, False)
        sin_turned = [bank("sin_turned%d" % i, b, P) for i, b in enumerate((6, 1))]
        for i in range(BLOCKS):
            nc.tensor.transpose(sin_turned[i][:], sin[QT][:, i * P : (i + 1) * P], identity[:])
        late = keep.tile([P, 5, Q], F32, name="late", tag="sin%d" % QT)
        finish(nc.gpsimd, fresh("res_p0"), 0, QP, a[0, QP], t_p[0])

        def block_term(h, i):
            t = keep.tile([P, P], F32, name="tt%d%d" % (h, i))
            nc.vector.scalar_tensor_tensor(
                t[:], yt[QT][:, i, (1 - h) * P : (2 - h) * P], -1.0 if h == 0 else 1.0, sin_turned[i][:], MULT, MULT
            )
            nc.tensor.matmul(
                sums[h, QT][:, i * P : (i + 1) * P], t[:], identity[:], is_transpose=True, start=False, stop=(i == BLOCKS - 1)
            )

        block_term(0, 0)
        block_term(1, 0)
        block_term(0, 1)
        t_a1 = product(late[:, 0, :], y[R1][:, 0, :], sin[R1])
        block_term(1, 1)
        finish(nc.vector, late[:, 4, :], 1, QP, parked[:], t_p[1])
        finish_turned(0, QT, "yt")
        joint_hi = keep.tile([P, 2 * Q], F32, name="joint_hi")
        nc.scalar.copy(out=joint_hi[:, :Q], in_=sums[1, QT][:])
        nc.gpsimd.tensor_tensor(joint_hi[:, Q:], a[1, R1], t_a1, ADD)
        nc.sync.dma_start(out=out[P:, QT * Q : (R1 + 1) * Q], in_=joint_hi[:])
        t_a0 = product(late[:, 1, :], y[R1][:, 1, :], sin[R1])
        joint_lo = keep.tile([P, 2 * Q], F32, name="joint_lo")
        nc.gpsimd.tensor_tensor(joint_lo[:, :Q], a[0, R1], t_a0, SUB)
        t_b1 = product(late[:, 2, :], y[R2][:, 0, :], sin[R2])
        t_b0 = product(late[:, 3, :], y[R2][:, 1, :], sin[R2])
        finish(nc.vector, fresh("res_b1"), 1, R2, a[1, R2], t_b1)
        nc.vector.tensor_tensor(joint_lo[:, Q:], a[0, R2], t_b0, SUB)
        nc.sync.dma_start(out=out[:P, R1 * Q :], in_=joint_lo[:])
